import numpy as np
import ml_dtypes


def mxq(x, axis, fmt="e4m3"):
    dtype, down = {"e4m3": (ml_dtypes.float8_e4m3fn, 7), "e5m2": (ml_dtypes.float8_e5m2, 14)}[fmt]
    v = np.moveaxis(np.asarray(x, np.float32).astype(ml_dtypes.bfloat16).astype(np.float64), axis, -1)
    blocks = v.reshape(v.shape[:-1] + (-1, 32))
    amax = np.abs(blocks).max(-1, keepdims=True)
    byte = np.maximum(np.where(amax > 0, np.frexp(amax)[1] - 1 + 127, 0) - down, 1)
    scale = np.exp2(byte - 127.0)
    codes = (blocks / scale).astype(np.float32).astype(dtype).astype(np.float64)
    return np.moveaxis((codes * scale).reshape(v.shape), -1, axis)


WIDE = False


def mx_kscale(k):
    if not WIDE:
        return np.ones(k)
    levels = np.array([10, -10, 5, -5, 0])
    if k % 512:
        return np.exp2(np.random.permutation(np.resize(levels, k // 32))).repeat(32)
    a = np.empty((k // 512, 16))
    for p in range(k // 512):
        a[p, :8] = np.random.permutation(np.resize(levels, 8))
        for g in range(8):
            far = levels[np.abs(levels - a[p, g]) >= 10]
            a[p, g + 8] = far[np.random.randint(len(far))]
    return np.exp2(a.ravel()).repeat(32)


def f64(x):
    return np.asarray(x).astype(np.float64)


def striped(idx):
    return np.tile(idx.reshape(-1, 16).T, (8, 1)).astype(np.uint16)


def unstriped(offs):
    return offs[:16].T.reshape(-1).astype(np.int64)


def pack_weight(w):
    k, n = w.shape
    w = f64(np.asarray(w, np.float32).astype(ml_dtypes.bfloat16)).reshape(k // 32, 32, n)
    amax = np.abs(w).max(1)
    byte = np.clip(np.where(amax > 0, np.frexp(amax)[1] - 1 + 127 - 7, 1), 1, 254)
    scaled = (w * np.exp2(127.0 - byte)[:, None, :]).reshape(k, n).astype(np.float32)
    words = np.ascontiguousarray(scaled.reshape(k // 512, 128, 4, n).transpose(0, 1, 3, 2)).astype(ml_dtypes.float8_e4m3fn).view(np.uint8)
    return words, np.ascontiguousarray(byte.astype(np.uint8).reshape(k // 512, 16, n))


def unpack_weight(words, scales):
    g, p, n, _ = words.shape
    vals = np.ascontiguousarray(words).view(ml_dtypes.float8_e4m3fn).astype(np.float64) * np.repeat(np.exp2(scales.astype(np.float64) - 127.0), 8, axis=1)[..., None]
    return vals.transpose(0, 1, 3, 2).reshape(g * 512, n)


K, T, S, H, N = 1024, 1024, 512, 512, 256


def setup_inputs():
    n = np.random.standard_normal
    s = mx_kscale(K)[:, None]
    u = mx_kscale(H)
    packed_xT = pack_weight(n((K, T)) * s)
    return {
        "x_words": packed_xT[0],
        "x_scales": packed_xT[1],
        "w1": (n((K, H)) / np.sqrt(K) / s * u).astype(np.float32),
        "w2": (n((H, N)) / np.sqrt(H) / u[:, None]).astype(np.float32),
        "pe": (0.5 * n((H, T)) * u[:, None]).astype(np.float32),
        "offs": striped(np.random.permutation(T)[:S]),
    }


def reference(x_words, x_scales, w1, w2, pe, offs):
    xq = unpack_weight(x_words, x_scales)[:, unstriped(offs)]
    g = f64(pe)[:, unstriped(offs)]
    h = (mxq(f64(w1), 0, "e4m3").T @ xq) + g
    return mxq(f64(w2), 0, "e4m3").T @ mxq(h, 0, "e4m3")

@@ -1,0 +1,177 @@
+from contextlib import ExitStack
+
+import concourse.mybir as mybir
+
+K, T, S, H, N = 1024, 1024, 512, 512, 256
+FLOPS = 2 * K * H * S + 2 * H * N * S
+
+F32 = mybir.dt.float32
+BF16 = mybir.dt.bfloat16
+I32 = mybir.dt.int32
+U32 = mybir.dt.uint32
+U16 = mybir.dt.uint16
+U8 = mybir.dt.uint8
+FP8X4 = mybir.dt.float8_e4m3fn_x4
+ADD = mybir.AluOpType.add
+
+P = 128
+PACK = 4
+PASSES = K // (P * PACK)
+CHUNK = 128
+CHUNKS = S // CHUNK
+LIST_COLS = CHUNK // 16
+W1_VECTOR_M = 40
+
+
+def tile_picked_posadd_none_p_kernel(tc, x_words, x_scales, w1, w2, pe, offs, out):
+    nc = tc.nc
+    with ExitStack() as ctx:
+        keep = ctx.enter_context(tc.tile_pool(name="keep", bufs=1))
+        psum = ctx.enter_context(tc.psum_pool(name="psum", bufs=1))
+
+        offsets = keep.tile([P, S // 16], U16, name="offsets")
+        x_table = [keep.tile([P, T], I32, name=f"x_table{z}", align_bytes=64) for z in range(PASSES)]
+        scale_table = keep.tile([P, T], U8, name="scale_table", align_bytes=64)
+        pieces = [(0, 0, P), (1, 0, P // 2), (1, P // 2, P)]
+        w1_raw = [keep.tile([P, PACK, (hi - lo) * PACK], F32, name=f"w1_raw{u}", align_bytes=64) for u, (z, lo, hi) in enumerate(pieces)]
+        pe_table = [keep.tile([P, T], F32, name=f"pe_table{t}", align_bytes=64) for t in range(PACK)]
+        w2_raw = keep.tile([P, PACK, N], F32, name="w2_raw", align_bytes=64)
+
+        def load_x(z):
+            nc.sync.dma_start(out=x_table[z][:], in_=x_words[z].rearrange("p c r -> p (c r)").bitcast(I32))
+
+        def load_w1(u):
+            z, lo, hi = pieces[u]
+            nc.sync.dma_start(out=w1_raw[u][:], in_=w1[z * P * PACK : (z + 1) * P * PACK, lo * PACK : hi * PACK].rearrange("(p j) c -> p j c", j=PACK))
+
+        nc.vector.memset(scale_table[:].bitcast(I32), 0)
+        load_x(0)
+        nc.sync.dma_start(offsets[:], offs)
+        load_w1(0)
+        for q in range(4):
+            nc.scalar.dma_start(
+                out=scale_table[32 * q : 32 * q + 4 * PASSES, :].bitcast(I32),
+                in_=x_scales[:, 4 * q : 4 * q + 4, :].bitcast(I32),
+            )
+        load_x(1)
+        load_w1(1)
+        pe_rows = pe.rearrange("(p t) c -> t p c", t=PACK)
+        for t in range(PACK):
+            nc.sync.dma_start(out=pe_table[t][:], in_=pe_rows[t])
+            if t == 0:
+                load_w1(2)
+        nc.sync.dma_start(out=w2_raw[:], in_=w2.rearrange("(p j) n -> p j n", j=PACK))
+
+        x_codes = [keep.tile([P, S], U32, name=f"x_codes{z}", align_bytes=64) for z in range(PASSES)]
+        x_planes = keep.tile([P, S], U8, name="x_planes", align_bytes=64)
+        w1_codes = [keep.tile([P, H], U32, name=f"w1_codes{z}", align_bytes=64) for z in range(PASSES)]
+        w1_planes = [keep.tile([P, H], U8, name=f"w1_planes{z}", align_bytes=64) for z in range(PASSES)]
+        picked = keep.tile([P, PACK, S], F32, name="picked", align_bytes=64)
+
+        def gather_pe(t):
+            nc.vector.tensor_copy(picked[:, t, :], pe_table[t][:].indirect(offsets[:]))
+
+        def quantize_w1(u, vector_m):
+            z, lo, hi = pieces[u]
+            grouped = keep.tile([P, PACK, hi - lo, PACK], BF16, name=f"w1_grouped{u}", align_bytes=64)
+            dst = grouped[:].rearrange("p t m j -> p m j t")
+            src = w1_raw[u][:].rearrange("p j (m t) -> p m j t", t=PACK)
+            if vector_m:
+                nc.vector.tensor_copy(out=dst[:, :vector_m], in_=src[:, :vector_m])
+            nc.scalar.copy(out=dst[:, vector_m:], in_=src[:, vector_m:])
+            if hi - lo == P:
+                nc.vector.quantize_mx(out=w1_codes[z][:].bitcast(FP8X4), scales=w1_planes[z][:], in_=grouped[:].rearrange("p t m j -> p (t m j)"))
+            else:
+                for t in range(PACK):
+                    cols = slice(t * P + lo, t * P + hi)
+                    nc.vector.quantize_mx(out=w1_codes[z][:, cols].bitcast(FP8X4), scales=w1_planes[z][:, cols], in_=grouped[:, t].rearrange("p m j -> p (m j)"))
+
+        nc.vector.tensor_copy(x_planes[:], scale_table[:].indirect(offsets[:]))
+        nc.vector.tensor_copy(x_codes[0][:], x_table[0][:].bitcast(U32).indirect(offsets[:]))
+        nc.vector.tensor_copy(x_codes[1][:], x_table[1][:].bitcast(U32).indirect(offsets[:]))
+        quantize_w1(0, 0)
+        quantize_w1(1, 0)
+        gather_pe(0)
+        quantize_w1(2, W1_VECTOR_M)
+
+        banks = []
+        for c in range(CHUNKS):
+            cols = slice(c * CHUNK, (c + 1) * CHUNK)
+            bank = psum.tile([P, PACK, CHUNK], F32, name=f"first{c}")
+            for t in range(PACK):
+                rows = slice(t * P, (t + 1) * P)
+                for z in range(PASSES):
+                    nc.tensor.matmul_mx(
+                        out=bank[:, t, :],
+                        lhsT=w1_codes[z][:, rows].bitcast(FP8X4),
+                        lhsT_scale=w1_planes[z][:, rows],
+                        rhs=x_codes[z][:, cols].bitcast(FP8X4),
+                        rhs_scale=x_planes[4 * z :, cols],
+                        start=(z == 0),
+                        stop=(z == PASSES - 1),
+                    )
+            banks.append(bank)
+
+        for t in range(1, PACK - 1):
+            gather_pe(t)
+
+        w2_grouped = keep.tile([P, N, PACK], BF16, name="w2_grouped", tag="late", align_bytes=64)
+        nc.scalar.copy(
+            out=w2_grouped[:].rearrange("p (c i) j -> p c j i", i=4),
+            in_=w2_raw[:].rearrange("p j (c i) -> p c j i", i=4),
+        )
+        w2_codes = keep.tile([P, N], U32, name="w2_codes", align_bytes=64)
+        w2_planes = keep.tile([P, N], U8, name="w2_planes", align_bytes=64)
+
+        h_grouped = {}
+
+        def gather_last(c):
+            nc.vector.tensor_copy(
+                picked[:, PACK - 1, c * CHUNK : (c + 1) * CHUNK],
+                pe_table[PACK - 1][:].indirect(offsets[:, c * LIST_COLS : (c + 1) * LIST_COLS]),
+            )
+
+        def add(c):
+            h_grouped[c] = keep.tile([P, CHUNK, PACK], BF16, name=f"h_grouped{c}", tag="late" if c == 2 else f"h_grouped{c}", align_bytes=64)
+            nc.vector.tensor_tensor(
+                h_grouped[c][:].rearrange("p (c i) t -> p c t i", i=4),
+                banks[c][:].rearrange("p t (c i) -> p c t i", i=4),
+                picked[:, :, c * CHUNK : (c + 1) * CHUNK].rearrange("p t (c i) -> p c t i", i=4),
+                ADD,
+            )
+
+        out_rows = out.rearrange("(a p) s -> p a s", p=P)
+
+        def second(c):
+            codes = keep.tile([P, CHUNK], U32, name=f"h_codes{c}", align_bytes=64)
+            planes = keep.tile([P, CHUNK], U8, name=f"h_planes{c}", align_bytes=64)
+            nc.vector.quantize_mx(out=codes[:].bitcast(FP8X4), scales=planes[:], in_=h_grouped[c][:].rearrange("p s t -> p (s t)"))
+            bank = psum.tile([P, N // P, CHUNK], F32, name=f"second{c}")
+            for a in range(N // P):
+                rows = slice(a * P, (a + 1) * P)
+                nc.tensor.matmul_mx(
+                    out=bank[:, a, :],
+                    lhsT=w2_codes[:, rows].bitcast(FP8X4),
+                    lhsT_scale=w2_planes[:, rows],
+                    rhs=codes[:].bitcast(FP8X4),
+                    rhs_scale=planes[:],
+                    start=True,
+                    stop=True,
+                )
+            result = keep.tile([P, N // P, CHUNK], F32, name=f"result{c}", align_bytes=64)
+            nc.scalar.copy(out=result[:], in_=bank[:])
+            nc.sync.dma_start(out=out_rows[:, :, c * CHUNK : (c + 1) * CHUNK], in_=result[:])
+
+        gather_last(0)
+        gather_last(1)
+        add(0)
+        gather_last(2)
+        add(1)
+        nc.vector.quantize_mx(out=w2_codes[:].bitcast(FP8X4), scales=w2_planes[:], in_=w2_grouped[:].rearrange("p n j -> p (n j)"))
+        second(0)
+        gather_last(3)
+        second(1)
+        add(2)
+        add(3)
+        second(2)
+        second(3)

@@ -17,10 +17,14 @@ ADD = mybir.AluOpType.add
 P = 128
 PACK = 4
 PASSES = K // (P * PACK)
+QUADRANT = 32
+SCALE_ROWS = 4
+ENTRIES_PER_COLUMN = 16
+RUN = 4
 CHUNK = 128
 CHUNKS = S // CHUNK
-LIST_COLS = CHUNK // 16
-W1_VECTOR_M = 40
+OUT_TILES = N // P
+ALIGN = 64
 
 
 def tile_picked_posadd_none_p_kernel(tc, x_words, x_scales, w1, w2, pe, offs, out):
@@ -29,149 +33,166 @@ def tile_picked_posadd_none_p_kernel(tc, x_words, x_scales, w1, w2, pe, offs, ou
         keep = ctx.enter_context(tc.tile_pool(name="keep", bufs=1))
         psum = ctx.enter_context(tc.psum_pool(name="psum", bufs=1))
 
-        offsets = keep.tile([P, S // 16], U16, name="offsets")
-        x_table = [keep.tile([P, T], I32, name=f"x_table{z}", align_bytes=64) for z in range(PASSES)]
-        scale_table = keep.tile([P, T], U8, name="scale_table", align_bytes=64)
-        pieces = [(0, 0, P), (1, 0, P // 2), (1, P // 2, P)]
-        w1_raw = [keep.tile([P, PACK, (hi - lo) * PACK], F32, name=f"w1_raw{u}", align_bytes=64) for u, (z, lo, hi) in enumerate(pieces)]
-        pe_table = [keep.tile([P, T], F32, name=f"pe_table{t}", align_bytes=64) for t in range(PACK)]
-        w2_raw = keep.tile([P, PACK, N], F32, name="w2_raw", align_bytes=64)
+        offsets = keep.tile([P, S // ENTRIES_PER_COLUMN], U16, name="offsets")
+        x_table = [keep.tile([P, T], I32, name=f"x_table{z}", align_bytes=ALIGN) for z in range(PASSES)]
+        scale_table = keep.tile([P, T], U8, name="scale_table", align_bytes=ALIGN)
+        w1_raw = [keep.tile([P, PACK, H], F32, name=f"w1_raw{z}", align_bytes=ALIGN) for z in range(PASSES)]
+        pe_table = [keep.tile([P, T], F32, name=f"pe_table{t}", align_bytes=ALIGN) for t in range(PACK)]
+        w2_raw = keep.tile([P, PACK, N], F32, name="w2_raw", align_bytes=ALIGN)
+
+        def entries(cols):
+            return offsets[:, cols.start // ENTRIES_PER_COLUMN : cols.stop // ENTRIES_PER_COLUMN]
 
         def load_x(z):
             nc.sync.dma_start(out=x_table[z][:], in_=x_words[z].rearrange("p c r -> p (c r)").bitcast(I32))
 
-        def load_w1(u):
-            z, lo, hi = pieces[u]
-            nc.sync.dma_start(out=w1_raw[u][:], in_=w1[z * P * PACK : (z + 1) * P * PACK, lo * PACK : hi * PACK].rearrange("(p j) c -> p j c", j=PACK))
+        def load_w1(z):
+            rows = w1[z * P * PACK : (z + 1) * P * PACK, :]
+            nc.sync.dma_start(out=w1_raw[z][:], in_=rows.rearrange("(p j) c -> p j c", j=PACK))
 
         nc.vector.memset(scale_table[:].bitcast(I32), 0)
         load_x(0)
         nc.sync.dma_start(offsets[:], offs)
-        load_w1(0)
-        for q in range(4):
-            nc.scalar.dma_start(
-                out=scale_table[32 * q : 32 * q + 4 * PASSES, :].bitcast(I32),
-                in_=x_scales[:, 4 * q : 4 * q + 4, :].bitcast(I32),
+        for q in range(P // QUADRANT):
+            nc.sync.dma_start(
+                out=scale_table[QUADRANT * q : QUADRANT * q + SCALE_ROWS * PASSES, :].bitcast(I32),
+                in_=x_scales[:, SCALE_ROWS * q : SCALE_ROWS * (q + 1), :].bitcast(I32),
             )
+        load_w1(0)
         load_x(1)
         load_w1(1)
-        pe_rows = pe.rearrange("(p t) c -> t p c", t=PACK)
+        pe_planes = pe.rearrange("(p t) c -> t p c", t=PACK)
         for t in range(PACK):
-            nc.sync.dma_start(out=pe_table[t][:], in_=pe_rows[t])
-            if t == 0:
-                load_w1(2)
-        nc.sync.dma_start(out=w2_raw[:], in_=w2.rearrange("(p j) n -> p j n", j=PACK))
+            if t == PACK // 2:
+                nc.sync.dma_start(out=w2_raw[:], in_=w2.rearrange("(p j) n -> p j n", j=PACK))
+            nc.sync.dma_start(out=pe_table[t][:], in_=pe_planes[t])
 
-        x_codes = [keep.tile([P, S], U32, name=f"x_codes{z}", align_bytes=64) for z in range(PASSES)]
-        x_planes = keep.tile([P, S], U8, name="x_planes", align_bytes=64)
-        w1_codes = [keep.tile([P, H], U32, name=f"w1_codes{z}", align_bytes=64) for z in range(PASSES)]
-        w1_planes = [keep.tile([P, H], U8, name=f"w1_planes{z}", align_bytes=64) for z in range(PASSES)]
-        picked = keep.tile([P, PACK, S], F32, name="picked", align_bytes=64)
+        w1_codes = [keep.tile([P, H], U32, name=f"w1_codes{z}", align_bytes=ALIGN) for z in range(PASSES)]
+        w1_scales = [keep.tile([P, H], U8, name=f"w1_scales{z}", align_bytes=ALIGN) for z in range(PASSES)]
 
-        def gather_pe(t):
-            nc.vector.tensor_copy(picked[:, t, :], pe_table[t][:].indirect(offsets[:]))
-
-        def quantize_w1(u, vector_m):
-            z, lo, hi = pieces[u]
-            grouped = keep.tile([P, PACK, hi - lo, PACK], BF16, name=f"w1_grouped{u}", align_bytes=64)
+        def group_w1(z):
+            grouped = keep.tile([P, PACK, P, PACK], BF16, name=f"w1_grouped{z}", tag=f"w1_grouped{z}", align_bytes=ALIGN)
             dst = grouped[:].rearrange("p t m j -> p m j t")
-            src = w1_raw[u][:].rearrange("p j (m t) -> p m j t", t=PACK)
-            if vector_m:
-                nc.vector.tensor_copy(out=dst[:, :vector_m], in_=src[:, :vector_m])
-            nc.scalar.copy(out=dst[:, vector_m:], in_=src[:, vector_m:])
-            if hi - lo == P:
-                nc.vector.quantize_mx(out=w1_codes[z][:].bitcast(FP8X4), scales=w1_planes[z][:], in_=grouped[:].rearrange("p t m j -> p (t m j)"))
-            else:
-                for t in range(PACK):
-                    cols = slice(t * P + lo, t * P + hi)
-                    nc.vector.quantize_mx(out=w1_codes[z][:, cols].bitcast(FP8X4), scales=w1_planes[z][:, cols], in_=grouped[:, t].rearrange("p m j -> p (m j)"))
+            src = w1_raw[z][:].rearrange("p j (m t) -> p m j t", t=PACK)
+            nc.vector.tensor_copy(out=dst[:, :, :, : PACK // 2], in_=src[:, :, :, : PACK // 2])
+            nc.scalar.copy(out=dst[:, :, :, PACK // 2 :], in_=src[:, :, :, PACK // 2 :])
+            return grouped
 
-        nc.vector.tensor_copy(x_planes[:], scale_table[:].indirect(offsets[:]))
-        nc.vector.tensor_copy(x_codes[0][:], x_table[0][:].bitcast(U32).indirect(offsets[:]))
-        nc.vector.tensor_copy(x_codes[1][:], x_table[1][:].bitcast(U32).indirect(offsets[:]))
-        quantize_w1(0, 0)
-        quantize_w1(1, 0)
-        gather_pe(0)
-        quantize_w1(2, W1_VECTOR_M)
-
-        banks = []
-        for c in range(CHUNKS):
-            cols = slice(c * CHUNK, (c + 1) * CHUNK)
-            bank = psum.tile([P, PACK, CHUNK], F32, name=f"first{c}")
-            for t in range(PACK):
-                rows = slice(t * P, (t + 1) * P)
-                for z in range(PASSES):
-                    nc.tensor.matmul_mx(
-                        out=bank[:, t, :],
-                        lhsT=w1_codes[z][:, rows].bitcast(FP8X4),
-                        lhsT_scale=w1_planes[z][:, rows],
-                        rhs=x_codes[z][:, cols].bitcast(FP8X4),
-                        rhs_scale=x_planes[4 * z :, cols],
-                        start=(z == 0),
-                        stop=(z == PASSES - 1),
-                    )
-            banks.append(bank)
-
-        for t in range(1, PACK - 1):
-            gather_pe(t)
-
-        w2_grouped = keep.tile([P, N, PACK], BF16, name="w2_grouped", tag="late", align_bytes=64)
-        nc.scalar.copy(
-            out=w2_grouped[:].rearrange("p (c i) j -> p c j i", i=4),
-            in_=w2_raw[:].rearrange("p j (c i) -> p c j i", i=4),
+        x_codes0 = keep.tile([P, S], U32, name="x_codes0", align_bytes=ALIGN)
+        x_picked_scales = keep.tile([P, S], U8, name="x_picked_scales", align_bytes=ALIGN)
+        nc.vector.tensor_copy(x_codes0[:], x_table[0][:].bitcast(U32).indirect(offsets[:]))
+        nc.vector.tensor_copy(x_picked_scales[:], scale_table[:].indirect(offsets[:]))
+        w1_grouped0 = group_w1(0)
+        nc.vector.quantize_mx(
+            out=w1_codes[0][:].bitcast(FP8X4),
+            scales=w1_scales[0][:],
+            in_=w1_grouped0[:].rearrange("p t m j -> p (t m j)"),
         )
-        w2_codes = keep.tile([P, N], U32, name="w2_codes", align_bytes=64)
-        w2_planes = keep.tile([P, N], U8, name="w2_planes", align_bytes=64)
+        x_codes1 = keep.tile([P, S], U32, name="x_codes1", tag="w1_grouped0", align_bytes=ALIGN)
+        nc.vector.tensor_copy(x_codes1[:], x_table[1][:].bitcast(U32).indirect(offsets[:]))
+        x_codes = [x_codes0, x_codes1]
+        w1_grouped1 = group_w1(1)
 
-        h_grouped = {}
+        plane_banks = [psum.tile([P, S], F32, name=f"plane_bank{t}", tag=f"plane_bank{t}") for t in range(PACK)]
 
-        def gather_last(c):
-            nc.vector.tensor_copy(
-                picked[:, PACK - 1, c * CHUNK : (c + 1) * CHUNK],
-                pe_table[PACK - 1][:].indirect(offsets[:, c * LIST_COLS : (c + 1) * LIST_COLS]),
+        def first_product(t, z):
+            cols = slice(t * P, (t + 1) * P)
+            nc.tensor.matmul_mx(
+                out=plane_banks[t][:],
+                lhsT=w1_codes[z][:, cols].bitcast(FP8X4),
+                lhsT_scale=w1_scales[z][:, cols],
+                rhs=x_codes[z][:].bitcast(FP8X4),
+                rhs_scale=x_picked_scales[SCALE_ROWS * z :, :],
+                start=(z == 0),
+                stop=(z == PASSES - 1),
             )
 
-        def add(c):
-            h_grouped[c] = keep.tile([P, CHUNK, PACK], BF16, name=f"h_grouped{c}", tag="late" if c == 2 else f"h_grouped{c}", align_bytes=64)
-            nc.vector.tensor_tensor(
-                h_grouped[c][:].rearrange("p (c i) t -> p c t i", i=4),
-                banks[c][:].rearrange("p t (c i) -> p c t i", i=4),
-                picked[:, :, c * CHUNK : (c + 1) * CHUNK].rearrange("p t (c i) -> p c t i", i=4),
-                ADD,
+        for t in range(PACK):
+            first_product(t, 0)
+
+        h = keep.tile([P, PACK, S], F32, name="h", align_bytes=ALIGN)
+        last_plane = h[:, PACK - 1, :]
+
+        halves = [slice(0, S // 2), slice(S // 2, S)]
+        whole = [slice(0, S)]
+        products = []
+        for t in range(PACK):
+            cols = slice(t * P, (t + 1) * P)
+            nc.vector.quantize_mx(
+                out=w1_codes[1][:, cols].bitcast(FP8X4),
+                scales=w1_scales[1][:, cols],
+                in_=w1_grouped1[:, t].rearrange("p m j -> p (m j)"),
             )
+            first_product(t, 1)
+            product = last_plane if t == 0 else keep.tile([P, S], F32, name=f"product{t}", align_bytes=ALIGN)
+            for part in halves if t == 0 else whole:
+                nc.scalar.copy(out=product[:, part], in_=plane_banks[t][:, part])
+            products.append(product)
 
-        out_rows = out.rearrange("(a p) s -> p a s", p=P)
+        def add_pe(t, part):
+            nc.vector.tensor_tensor(h[:, t, part], pe_table[t][:].indirect(entries(part)), products[t][:, part], ADD)
 
-        def second(c):
-            codes = keep.tile([P, CHUNK], U32, name=f"h_codes{c}", align_bytes=64)
-            planes = keep.tile([P, CHUNK], U8, name=f"h_planes{c}", align_bytes=64)
-            nc.vector.quantize_mx(out=codes[:].bitcast(FP8X4), scales=planes[:], in_=h_grouped[c][:].rearrange("p s t -> p (s t)"))
-            bank = psum.tile([P, N // P, CHUNK], F32, name=f"second{c}")
-            for a in range(N // P):
-                rows = slice(a * P, (a + 1) * P)
+        for t in range(PACK - 1):
+            for part in halves if t == 0 else whole:
+                add_pe(t, part)
+
+        w2_grouped = last_plane.bitcast(BF16)
+        nc.scalar.copy(
+            out=w2_grouped.rearrange("p (c i j) -> p c j i", i=RUN, j=PACK),
+            in_=w2_raw[:].rearrange("p j (c i) -> p c j i", i=RUN),
+        )
+        w2_codes = keep.tile([P, N], U32, name="w2_codes", align_bytes=ALIGN)
+        w2_scales = keep.tile([P, N], U8, name="w2_scales", align_bytes=ALIGN)
+        nc.vector.quantize_mx(out=w2_codes[:].bitcast(FP8X4), scales=w2_scales[:], in_=w2_grouped)
+
+        chunks = [slice(c * CHUNK, (c + 1) * CHUNK) for c in range(CHUNKS)]
+        out_tiles = out.rearrange("(a p) s -> p a s", p=P)
+
+        def group_h(c, copy, place):
+            grouped = keep.tile([P, CHUNK, PACK], BF16, name=f"h_grouped{c}", tag=f"h_grouped{place}", align_bytes=ALIGN)
+            copy(
+                out=grouped[:].rearrange("p (c i) t -> p c t i", i=RUN),
+                in_=h[:, :, chunks[c]].rearrange("p t (c i) -> p c t i", i=RUN),
+            )
+            return grouped
+
+        def second_product(c, grouped, sums):
+            codes = keep.tile([P, CHUNK], U32, name=f"h_codes{c}", align_bytes=ALIGN)
+            scales = keep.tile([P, CHUNK], U8, name=f"h_scales{c}", align_bytes=ALIGN)
+            nc.vector.quantize_mx(out=codes[:].bitcast(FP8X4), scales=scales[:], in_=grouped[:].rearrange("p s t -> p (s t)"))
+            for a in range(OUT_TILES):
+                cols = slice(a * P, (a + 1) * P)
                 nc.tensor.matmul_mx(
-                    out=bank[:, a, :],
-                    lhsT=w2_codes[:, rows].bitcast(FP8X4),
-                    lhsT_scale=w2_planes[:, rows],
+                    out=sums[a],
+                    lhsT=w2_codes[:, cols].bitcast(FP8X4),
+                    lhsT_scale=w2_scales[:, cols],
                     rhs=codes[:].bitcast(FP8X4),
-                    rhs_scale=planes[:],
+                    rhs_scale=scales[:],
                     start=True,
                     stop=True,
                 )
-            result = keep.tile([P, N // P, CHUNK], F32, name=f"result{c}", align_bytes=64)
-            nc.scalar.copy(out=result[:], in_=bank[:])
-            nc.sync.dma_start(out=out_rows[:, :, c * CHUNK : (c + 1) * CHUNK], in_=result[:])
 
-        gather_last(0)
-        gather_last(1)
-        add(0)
-        gather_last(2)
-        add(1)
-        nc.vector.quantize_mx(out=w2_codes[:].bitcast(FP8X4), scales=w2_planes[:], in_=w2_grouped[:].rearrange("p n j -> p (n j)"))
-        second(0)
-        gather_last(3)
-        second(1)
-        add(2)
-        add(3)
-        second(2)
-        second(3)
+        def finish(c, grouped):
+            result = keep.tile([P, OUT_TILES, CHUNK], F32, name=f"result{c}", align_bytes=ALIGN)
+            bank = psum.tile([P, OUT_TILES, CHUNK], F32, name=f"out_bank{c}")
+            second_product(c, grouped, [bank[:, a, :] for a in range(OUT_TILES)])
+            nc.scalar.copy(out=result[:], in_=bank[:])
+            nc.sync.dma_start(out=out_tiles[:, :, chunks[c]], in_=result[:])
+
+        def finish_last(c, grouped):
+            result = keep.tile([P, OUT_TILES, CHUNK], F32, name=f"result{c}", align_bytes=ALIGN)
+            banks = [psum.tile([P, CHUNK], F32, name=f"last_bank{a}", tag=f"plane_bank{a}") for a in range(OUT_TILES)]
+            second_product(c, grouped, [bank[:] for bank in banks])
+            nc.scalar.copy(out=result[:, 0, :], in_=banks[0][:])
+            nc.vector.tensor_copy(out=result[:, 1, :], in_=banks[1][:])
+            nc.sync.dma_start(out=out_tiles[:, :, chunks[c]], in_=result[:])
+
+        for part in chunks:
+            add_pe(PACK - 1, part)
+        last = CHUNKS - 1
+        h_grouped = [group_h(c, nc.scalar.copy, c) for c in range(last)]
+        finish(0, h_grouped[0])
+        finish(1, h_grouped[1])
+        last_grouped = group_h(last, nc.vector.tensor_copy, 1)
+        finish(2, h_grouped[2])
+        finish_last(last, last_grouped)

@@ -16,6 +16,7 @@ ADD = mybir.AluOpType.add
 
 P = 128
 PACK = 4
+PAIR = 2
 PASSES = K // (P * PACK)
 QUADRANT = 32
 SCALE_ROWS = 4
@@ -36,7 +37,8 @@ def tile_picked_posadd_none_p_kernel(tc, x_words, x_scales, w1, w2, pe, offs, ou
         offsets = keep.tile([P, S // ENTRIES_PER_COLUMN], U16, name="offsets")
         x_table = [keep.tile([P, T], I32, name=f"x_table{z}", align_bytes=ALIGN) for z in range(PASSES)]
         scale_table = keep.tile([P, T], U8, name="scale_table", align_bytes=ALIGN)
-        w1_raw = [keep.tile([P, PACK, H], F32, name=f"w1_raw{z}", align_bytes=ALIGN) for z in range(PASSES)]
+        w1_raw0 = keep.tile([P, PACK, H], F32, name="w1_raw0", align_bytes=ALIGN)
+        w1_raw1 = [keep.tile([P, PAIR, H], F32, name=f"w1_raw1_{u}", align_bytes=ALIGN) for u in range(PACK // PAIR)]
         pe_table = [keep.tile([P, T], F32, name=f"pe_table{t}", align_bytes=ALIGN) for t in range(PACK)]
         w2_raw = keep.tile([P, PACK, N], F32, name="w2_raw", align_bytes=ALIGN)
 
@@ -46,9 +48,8 @@ def tile_picked_posadd_none_p_kernel(tc, x_words, x_scales, w1, w2, pe, offs, ou
         def load_x(z):
             nc.sync.dma_start(out=x_table[z][:], in_=x_words[z].rearrange("p c r -> p (c r)").bitcast(I32))
 
-        def load_w1(z):
-            rows = w1[z * P * PACK : (z + 1) * P * PACK, :]
-            nc.sync.dma_start(out=w1_raw[z][:], in_=rows.rearrange("(p j) c -> p j c", j=PACK))
+        w1_rows = w1.rearrange("(z p j) c -> z p j c", z=PASSES, j=PACK)
+        pe_planes = pe.rearrange("(p t) c -> t p c", t=PACK)
 
         nc.vector.memset(scale_table[:].bitcast(I32), 0)
         load_x(0)
@@ -58,47 +59,50 @@ def tile_picked_posadd_none_p_kernel(tc, x_words, x_scales, w1, w2, pe, offs, ou
                 out=scale_table[QUADRANT * q : QUADRANT * q + SCALE_ROWS * PASSES, :].bitcast(I32),
                 in_=x_scales[:, SCALE_ROWS * q : SCALE_ROWS * (q + 1), :].bitcast(I32),
             )
-        load_w1(0)
+        nc.sync.dma_start(out=w1_raw0[:], in_=w1_rows[0])
         load_x(1)
-        load_w1(1)
-        pe_planes = pe.rearrange("(p t) c -> t p c", t=PACK)
+        for u in range(PACK // PAIR):
+            nc.sync.dma_start(out=w1_raw1[u][:], in_=w1_rows[1][:, PAIR * u : PAIR * (u + 1), :])
         for t in range(PACK):
-            if t == PACK // 2:
+            if t == PACK - 1:
                 nc.sync.dma_start(out=w2_raw[:], in_=w2.rearrange("(p j) n -> p j n", j=PACK))
             nc.sync.dma_start(out=pe_table[t][:], in_=pe_planes[t])
 
         w1_codes = [keep.tile([P, H], U32, name=f"w1_codes{z}", align_bytes=ALIGN) for z in range(PASSES)]
         w1_scales = [keep.tile([P, H], U8, name=f"w1_scales{z}", align_bytes=ALIGN) for z in range(PASSES)]
+        w1_grouped = [keep.tile([P, PACK, P, PACK], BF16, name=f"w1_grouped{z}", tag=f"w1_grouped{z}", align_bytes=ALIGN) for z in range(PASSES)]
 
-        def group_w1(z):
-            grouped = keep.tile([P, PACK, P, PACK], BF16, name=f"w1_grouped{z}", tag=f"w1_grouped{z}", align_bytes=ALIGN)
-            dst = grouped[:].rearrange("p t m j -> p m j t")
-            src = w1_raw[z][:].rearrange("p j (m t) -> p m j t", t=PACK)
-            nc.vector.tensor_copy(out=dst[:, :, :, : PACK // 2], in_=src[:, :, :, : PACK // 2])
-            nc.scalar.copy(out=dst[:, :, :, PACK // 2 :], in_=src[:, :, :, PACK // 2 :])
-            return grouped
+        def group_w1(copy, z, raw, rows, planes):
+            dst = w1_grouped[z][:].rearrange("p t m j -> p m j t")
+            src = raw[:].rearrange("p j (m t) -> p m j t", t=PACK)
+            copy(out=dst[:, :, rows, planes], in_=src[:, :, :, planes])
 
-        x_codes0 = keep.tile([P, S], U32, name="x_codes0", align_bytes=ALIGN)
+        def quantise_w1(z, planes):
+            cols = slice(planes.start * P, planes.stop * P)
+            nc.vector.quantize_mx(
+                out=w1_codes[z][:, cols].bitcast(FP8X4),
+                scales=w1_scales[z][:, cols],
+                in_=w1_grouped[z][:, planes].rearrange("p t m j -> p (t m j)"),
+            )
+
+        x_codes = [keep.tile([P, S], U32, name=f"x_codes{z}", align_bytes=ALIGN) for z in range(PASSES)]
         x_picked_scales = keep.tile([P, S], U8, name="x_picked_scales", align_bytes=ALIGN)
-        nc.vector.tensor_copy(x_codes0[:], x_table[0][:].bitcast(U32).indirect(offsets[:]))
+        nc.vector.tensor_copy(x_codes[0][:], x_table[0][:].bitcast(U32).indirect(offsets[:]))
         nc.vector.tensor_copy(x_picked_scales[:], scale_table[:].indirect(offsets[:]))
-        w1_grouped0 = group_w1(0)
-        nc.vector.quantize_mx(
-            out=w1_codes[0][:].bitcast(FP8X4),
-            scales=w1_scales[0][:],
-            in_=w1_grouped0[:].rearrange("p t m j -> p (t m j)"),
-        )
-        x_codes1 = keep.tile([P, S], U32, name="x_codes1", tag="w1_grouped0", align_bytes=ALIGN)
-        nc.vector.tensor_copy(x_codes1[:], x_table[1][:].bitcast(U32).indirect(offsets[:]))
-        x_codes = [x_codes0, x_codes1]
-        w1_grouped1 = group_w1(1)
 
-        plane_banks = [psum.tile([P, S], F32, name=f"plane_bank{t}", tag=f"plane_bank{t}") for t in range(PACK)]
+        low, high, every = slice(0, PAIR), slice(PAIR, PACK), slice(0, PACK)
+        group_w1(nc.vector.tensor_copy, 0, w1_raw0, every, low)
+        group_w1(nc.scalar.copy, 0, w1_raw0, every, high)
+        quantise_w1(0, low)
+        nc.vector.tensor_copy(x_codes[1][:], x_table[1][:].bitcast(U32).indirect(offsets[:]))
+        quantise_w1(0, high)
+
+        banks = [psum.tile([P, S], F32, name=f"plane_bank{t}", tag=f"bank{t}") for t in range(PACK)]
 
         def first_product(t, z):
             cols = slice(t * P, (t + 1) * P)
             nc.tensor.matmul_mx(
-                out=plane_banks[t][:],
+                out=banks[t][:],
                 lhsT=w1_codes[z][:, cols].bitcast(FP8X4),
                 lhsT_scale=w1_scales[z][:, cols],
                 rhs=x_codes[z][:].bitcast(FP8X4),
@@ -110,56 +114,59 @@ def tile_picked_posadd_none_p_kernel(tc, x_words, x_scales, w1, w2, pe, offs, ou
         for t in range(PACK):
             first_product(t, 0)
 
-        h = keep.tile([P, PACK, S], F32, name="h", align_bytes=ALIGN)
-        last_plane = h[:, PACK - 1, :]
+        group_w1(nc.scalar.copy, 1, w1_raw1[0], low, low)
+        group_w1(nc.vector.tensor_copy, 1, w1_raw1[0], low, high)
+        group_w1(nc.vector.tensor_copy, 1, w1_raw1[1], high, low)
+        group_w1(nc.scalar.copy, 1, w1_raw1[1], high, high)
+        quantise_w1(1, low)
+        quantise_w1(1, high)
 
+        h_store = keep.tile([P, PACK * S + CHUNK], F32, name="h_store", align_bytes=ALIGN)
+        h = h_store[:, : PACK * S].rearrange("p (t s) -> p t s", t=PACK)
+
+        whole = slice(0, S)
         halves = [slice(0, S // 2), slice(S // 2, S)]
-        whole = [slice(0, S)]
-        products = []
-        for t in range(PACK):
-            cols = slice(t * P, (t + 1) * P)
-            nc.vector.quantize_mx(
-                out=w1_codes[1][:, cols].bitcast(FP8X4),
-                scales=w1_scales[1][:, cols],
-                in_=w1_grouped1[:, t].rearrange("p m j -> p (m j)"),
-            )
+        pe_picked = w1_grouped[1][:, low].rearrange("p t m j -> p (t m j)").bitcast(F32)
+        for part in halves:
+            nc.vector.tensor_copy(pe_picked[:, part], pe_table[0][:].indirect(entries(part)))
+        first_product(0, 1)
+        for part in halves:
+            nc.vector.tensor_tensor(h[:, 0, part], banks[0][:, part], pe_picked[:, part], ADD)
+
+        products = {}
+        for t in range(1, PACK):
+            products[t] = keep.tile([P, S], F32, name=f"product{t}", tag=f"product{t}", align_bytes=ALIGN)
             first_product(t, 1)
-            product = last_plane if t == 0 else keep.tile([P, S], F32, name=f"product{t}", align_bytes=ALIGN)
-            for part in halves if t == 0 else whole:
-                nc.scalar.copy(out=product[:, part], in_=plane_banks[t][:, part])
-            products.append(product)
+            nc.scalar.copy(out=products[t][:], in_=banks[t][:])
 
         def add_pe(t, part):
             nc.vector.tensor_tensor(h[:, t, part], pe_table[t][:].indirect(entries(part)), products[t][:, part], ADD)
 
-        for t in range(PACK - 1):
-            for part in halves if t == 0 else whole:
-                add_pe(t, part)
+        for t in range(1, PACK - 1):
+            add_pe(t, whole)
 
-        w2_grouped = last_plane.bitcast(BF16)
+        w2_grouped = keep.tile([P, N * PACK], BF16, name="w2_grouped", tag="product1", align_bytes=ALIGN)
         nc.scalar.copy(
-            out=w2_grouped.rearrange("p (c i j) -> p c j i", i=RUN, j=PACK),
+            out=w2_grouped[:].rearrange("p (c i j) -> p c j i", i=RUN, j=PACK),
             in_=w2_raw[:].rearrange("p j (c i) -> p c j i", i=RUN),
         )
         w2_codes = keep.tile([P, N], U32, name="w2_codes", align_bytes=ALIGN)
         w2_scales = keep.tile([P, N], U8, name="w2_scales", align_bytes=ALIGN)
-        nc.vector.quantize_mx(out=w2_codes[:].bitcast(FP8X4), scales=w2_scales[:], in_=w2_grouped)
+        nc.vector.quantize_mx(out=w2_codes[:].bitcast(FP8X4), scales=w2_scales[:], in_=w2_grouped[:])
 
         chunks = [slice(c * CHUNK, (c + 1) * CHUNK) for c in range(CHUNKS)]
         out_tiles = out.rearrange("(a p) s -> p a s", p=P)
 
-        def group_h(c, copy, place):
-            grouped = keep.tile([P, CHUNK, PACK], BF16, name=f"h_grouped{c}", tag=f"h_grouped{place}", align_bytes=ALIGN)
+        def group_h(c, copy, grouped):
             copy(
-                out=grouped[:].rearrange("p (c i) t -> p c t i", i=RUN),
+                out=grouped.rearrange("p (c i t) -> p c t i", i=RUN, t=PACK),
                 in_=h[:, :, chunks[c]].rearrange("p t (c i) -> p c t i", i=RUN),
             )
-            return grouped
 
         def second_product(c, grouped, sums):
             codes = keep.tile([P, CHUNK], U32, name=f"h_codes{c}", align_bytes=ALIGN)
             scales = keep.tile([P, CHUNK], U8, name=f"h_scales{c}", align_bytes=ALIGN)
-            nc.vector.quantize_mx(out=codes[:].bitcast(FP8X4), scales=scales[:], in_=grouped[:].rearrange("p s t -> p (s t)"))
+            nc.vector.quantize_mx(out=codes[:].bitcast(FP8X4), scales=scales[:], in_=grouped)
             for a in range(OUT_TILES):
                 cols = slice(a * P, (a + 1) * P)
                 nc.tensor.matmul_mx(
@@ -181,18 +188,24 @@ def tile_picked_posadd_none_p_kernel(tc, x_words, x_scales, w1, w2, pe, offs, ou
 
         def finish_last(c, grouped):
             result = keep.tile([P, OUT_TILES, CHUNK], F32, name=f"result{c}", align_bytes=ALIGN)
-            banks = [psum.tile([P, CHUNK], F32, name=f"last_bank{a}", tag=f"plane_bank{a}") for a in range(OUT_TILES)]
-            second_product(c, grouped, [bank[:] for bank in banks])
-            nc.scalar.copy(out=result[:, 0, :], in_=banks[0][:])
-            nc.vector.tensor_copy(out=result[:, 1, :], in_=banks[1][:])
+            last_banks = [psum.tile([P, CHUNK], F32, name=f"last_bank{a}", tag=f"bank{a}") for a in range(OUT_TILES)]
+            second_product(c, grouped, [bank[:] for bank in last_banks])
+            nc.scalar.copy(out=result[:, 0, :], in_=last_banks[0][:])
+            nc.vector.tensor_copy(out=result[:, 1, :], in_=last_banks[1][:])
             nc.sync.dma_start(out=out_tiles[:, :, chunks[c]], in_=result[:])
 
-        for part in chunks:
-            add_pe(PACK - 1, part)
         last = CHUNKS - 1
-        h_grouped = [group_h(c, nc.scalar.copy, c) for c in range(last)]
-        finish(0, h_grouped[0])
-        finish(1, h_grouped[1])
-        last_grouped = group_h(last, nc.vector.tensor_copy, 1)
-        finish(2, h_grouped[2])
-        finish_last(last, last_grouped)
+        grouped = [h_store[:, PACK * S - CHUNK :].bitcast(BF16)]
+        for c in range(1, last):
+            tile = keep.tile([P, CHUNK * PACK], BF16, name=f"h_grouped{c}", tag=f"h_grouped{c}", align_bytes=ALIGN)
+            grouped.append(tile[:])
+        for c in range(last):
+            add_pe(PACK - 1, chunks[c])
+            group_h(c, nc.scalar.copy, grouped[c])
+        finish(0, grouped[0])
+        add_pe(PACK - 1, chunks[last])
+        finish(1, grouped[1])
+        last_grouped = keep.tile([P, CHUNK * PACK], BF16, name="h_grouped_last", tag="h_grouped1", align_bytes=ALIGN)
+        group_h(last, nc.vector.tensor_copy, last_grouped[:])
+        finish(2, grouped[2])
+        finish_last(last, last_grouped[:])

@@ -60,9 +60,9 @@ def tile_picked_posadd_none_p_kernel(tc, x_words, x_scales, w1, w2, pe, offs, ou
                 in_=x_scales[:, SCALE_ROWS * q : SCALE_ROWS * (q + 1), :].bitcast(I32),
             )
         nc.sync.dma_start(out=w1_raw0[:], in_=w1_rows[0])
-        load_x(1)
         for u in range(PACK // PAIR):
             nc.sync.dma_start(out=w1_raw1[u][:], in_=w1_rows[1][:, PAIR * u : PAIR * (u + 1), :])
+        load_x(1)
         for t in range(PACK):
             if t == PACK - 1:
                 nc.sync.dma_start(out=w2_raw[:], in_=w2.rearrange("(p j) n -> p j n", j=PACK))
@@ -94,53 +94,56 @@ def tile_picked_posadd_none_p_kernel(tc, x_words, x_scales, w1, w2, pe, offs, ou
         group_w1(nc.vector.tensor_copy, 0, w1_raw0, every, low)
         group_w1(nc.scalar.copy, 0, w1_raw0, every, high)
         quantise_w1(0, low)
-        nc.vector.tensor_copy(x_codes[1][:], x_table[1][:].bitcast(U32).indirect(offsets[:]))
-        quantise_w1(0, high)
-
-        banks = [psum.tile([P, S], F32, name=f"plane_bank{t}", tag=f"bank{t}") for t in range(PACK)]
-
-        def first_product(t, z):
-            cols = slice(t * P, (t + 1) * P)
-            nc.tensor.matmul_mx(
-                out=banks[t][:],
-                lhsT=w1_codes[z][:, cols].bitcast(FP8X4),
-                lhsT_scale=w1_scales[z][:, cols],
-                rhs=x_codes[z][:].bitcast(FP8X4),
-                rhs_scale=x_picked_scales[SCALE_ROWS * z :, :],
-                start=(z == 0),
-                stop=(z == PASSES - 1),
-            )
-
-        for t in range(PACK):
-            first_product(t, 0)
-
         group_w1(nc.scalar.copy, 1, w1_raw1[0], low, low)
         group_w1(nc.vector.tensor_copy, 1, w1_raw1[0], low, high)
+        quantise_w1(0, high)
         group_w1(nc.vector.tensor_copy, 1, w1_raw1[1], high, low)
         group_w1(nc.scalar.copy, 1, w1_raw1[1], high, high)
         quantise_w1(1, low)
         quantise_w1(1, high)
+        whole = slice(0, S)
+        halves = [slice(0, S // 2), slice(S // 2, S)]
+        for part in halves:
+            nc.vector.tensor_copy(x_codes[1][:, part], x_table[1][:].bitcast(U32).indirect(entries(part)))
+
+        stretches = [(0, halves[0]), (0, halves[1])] + [(t, whole) for t in range(1, PACK)]
+        banks = [
+            psum.tile([P, part.stop - part.start], F32, name=f"plane_bank{b}", tag=f"bank{b}")
+            for b, (t, part) in enumerate(stretches)
+        ]
+
+        def first_product(b, z):
+            t, part = stretches[b]
+            cols = slice(t * P, (t + 1) * P)
+            nc.tensor.matmul_mx(
+                out=banks[b][:],
+                lhsT=w1_codes[z][:, cols].bitcast(FP8X4),
+                lhsT_scale=w1_scales[z][:, cols],
+                rhs=x_codes[z][:, part].bitcast(FP8X4),
+                rhs_scale=x_picked_scales[SCALE_ROWS * z :, part],
+                start=(z == 0),
+                stop=(z == PASSES - 1),
+            )
+
+        for z in range(PASSES):
+            for b in range(len(stretches)):
+                first_product(b, z)
 
         h_store = keep.tile([P, PACK * S + CHUNK], F32, name="h_store", align_bytes=ALIGN)
         h = h_store[:, : PACK * S].rearrange("p (t s) -> p t s", t=PACK)
 
-        whole = slice(0, S)
-        halves = [slice(0, S // 2), slice(S // 2, S)]
-        pe_picked = w1_grouped[1][:, low].rearrange("p t m j -> p (t m j)").bitcast(F32)
-        for part in halves:
-            nc.vector.tensor_copy(pe_picked[:, part], pe_table[0][:].indirect(entries(part)))
-        first_product(0, 1)
-        for part in halves:
-            nc.vector.tensor_tensor(h[:, 0, part], banks[0][:, part], pe_picked[:, part], ADD)
-
-        products = {}
-        for t in range(1, PACK):
-            products[t] = keep.tile([P, S], F32, name=f"product{t}", tag=f"product{t}", align_bytes=ALIGN)
-            first_product(t, 1)
-            nc.scalar.copy(out=products[t][:], in_=banks[t][:])
+        products = [keep.tile([P, S], F32, name=f"product{t}", tag=f"product{t}", align_bytes=ALIGN) for t in range(PACK)]
+        for b, (t, part) in enumerate(stretches):
+            if b != 1:
+                nc.scalar.copy(out=products[t][:, part], in_=banks[b][:])
 
         def add_pe(t, part):
             nc.vector.tensor_tensor(h[:, t, part], pe_table[t][:].indirect(entries(part)), products[t][:, part], ADD)
+
+        pe_picked = keep.tile([P, S // 2], F32, name="pe_picked", align_bytes=ALIGN)
+        nc.vector.tensor_copy(pe_picked[:], pe_table[0][:].indirect(entries(halves[1])))
+        add_pe(0, halves[0])
+        nc.vector.tensor_tensor(h[:, 0, halves[1]], banks[1][:], pe_picked[:], ADD)
 
         for t in range(1, PACK - 1):
             add_pe(t, whole)
@@ -190,9 +193,10 @@ def tile_picked_posadd_none_p_kernel(tc, x_words, x_scales, w1, w2, pe, offs, ou
             result = keep.tile([P, OUT_TILES, CHUNK], F32, name=f"result{c}", align_bytes=ALIGN)
             last_banks = [psum.tile([P, CHUNK], F32, name=f"last_bank{a}", tag=f"bank{a}") for a in range(OUT_TILES)]
             second_product(c, grouped, [bank[:] for bank in last_banks])
-            nc.scalar.copy(out=result[:, 0, :], in_=last_banks[0][:])
-            nc.vector.tensor_copy(out=result[:, 1, :], in_=last_banks[1][:])
-            nc.sync.dma_start(out=out_tiles[:, :, chunks[c]], in_=result[:])
+            nc.vector.tensor_copy(out=result[:, 0, :], in_=last_banks[0][:])
+            nc.sync.dma_start(out=out_tiles[:, 0, chunks[c]], in_=result[:, 0, :])
+            nc.scalar.copy(out=result[:, 1, :], in_=last_banks[1][:])
+            nc.scalar.dma_start(out=out_tiles[:, 1, chunks[c]], in_=result[:, 1, :])
 
         last = CHUNKS - 1
         grouped = [h_store[:, PACK * S - CHUNK :].bitcast(BF16)]

@@ -132,39 +132,62 @@ def tile_picked_posadd_none_p_kernel(tc, x_words, x_scales, w1, w2, pe, offs, ou
         h_store = keep.tile([P, PACK * S + CHUNK], F32, name="h_store", align_bytes=ALIGN)
         h = h_store[:, : PACK * S].rearrange("p (t s) -> p t s", t=PACK)
 
-        products = [keep.tile([P, S], F32, name=f"product{t}", tag=f"product{t}", align_bytes=ALIGN) for t in range(PACK)]
-        for b, (t, part) in enumerate(stretches):
+        products = [keep.tile([P, S], F32, name=f"product{t}", tag=f"product{t}", align_bytes=ALIGN) for t in range(PACK - 1)]
+        for b, (t, part) in enumerate(stretches[:-1]):
             if b != 1:
                 nc.scalar.copy(out=products[t][:, part], in_=banks[b][:])
+        last_products = []
+        for u, part in enumerate(halves):
+            product = keep.tile([P, S // 2], F32, name=f"last_product{u}", tag=f"last_product{u}", align_bytes=ALIGN)
+            nc.scalar.copy(out=product[:], in_=banks[-1][:, part])
+            last_products.append(product)
 
         def add_pe(t, part):
-            nc.vector.tensor_tensor(h[:, t, part], pe_table[t][:].indirect(entries(part)), products[t][:, part], ADD)
+            if t < PACK - 1:
+                product = products[t][:, part]
+            else:
+                u, first = divmod(part.start, S // 2)
+                product = last_products[u][:, first : first + part.stop - part.start]
+            nc.vector.tensor_tensor(h[:, t, part], pe_table[t][:].indirect(entries(part)), product, ADD)
 
         pe_picked = keep.tile([P, S // 2], F32, name="pe_picked", align_bytes=ALIGN)
         nc.vector.tensor_copy(pe_picked[:], pe_table[0][:].indirect(entries(halves[1])))
         add_pe(0, halves[0])
         nc.vector.tensor_tensor(h[:, 0, halves[1]], banks[1][:], pe_picked[:], ADD)
 
-        for t in range(1, PACK - 1):
-            add_pe(t, whole)
+        chunks = [slice(c * CHUNK, (c + 1) * CHUNK) for c in range(CHUNKS)]
+        last = CHUNKS - 1
+        grouped = [h_store[:, PACK * S - CHUNK :].bitcast(BF16)]
+        for c in range(1, last):
+            tile = keep.tile([P, CHUNK * PACK], BF16, name=f"h_grouped{c}", tag=f"h_grouped{c}", align_bytes=ALIGN)
+            grouped.append(tile[:])
+
+        def group_h(c, copy, target, planes):
+            copy(
+                out=target.rearrange("p (c i t) -> p c t i", i=RUN, t=PACK)[:, :, planes, :],
+                in_=h[:, planes, chunks[c]].rearrange("p t (c i) -> p c t i", i=RUN),
+            )
+
+        every = slice(0, PACK)
+        add_pe(1, halves[0])
+        for c in range(CHUNKS // 2):
+            group_h(c, nc.scalar.copy, grouped[c], low)
+        add_pe(1, halves[1])
+        add_pe(2, whole)
 
         w2_grouped = keep.tile([P, N * PACK], BF16, name="w2_grouped", tag="product1", align_bytes=ALIGN)
         nc.scalar.copy(
             out=w2_grouped[:].rearrange("p (c i j) -> p c j i", i=RUN, j=PACK),
             in_=w2_raw[:].rearrange("p j (c i) -> p c j i", i=RUN),
         )
-        w2_codes = keep.tile([P, N], U32, name="w2_codes", align_bytes=ALIGN)
+
+        out_tiles = out.rearrange("(a p) s -> p a s", p=P)
+        for c in range(last):
+            add_pe(PACK - 1, chunks[c])
+            group_h(c, nc.scalar.copy, grouped[c], high if c < CHUNKS // 2 else every)
+        w2_codes = keep.tile([P, N], U32, name="w2_codes", tag="last_product0", align_bytes=ALIGN)
         w2_scales = keep.tile([P, N], U8, name="w2_scales", align_bytes=ALIGN)
         nc.vector.quantize_mx(out=w2_codes[:].bitcast(FP8X4), scales=w2_scales[:], in_=w2_grouped[:])
-
-        chunks = [slice(c * CHUNK, (c + 1) * CHUNK) for c in range(CHUNKS)]
-        out_tiles = out.rearrange("(a p) s -> p a s", p=P)
-
-        def group_h(c, copy, grouped):
-            copy(
-                out=grouped.rearrange("p (c i t) -> p c t i", i=RUN, t=PACK),
-                in_=h[:, :, chunks[c]].rearrange("p t (c i) -> p c t i", i=RUN),
-            )
 
         def second_product(c, grouped, sums):
             codes = keep.tile([P, CHUNK], U32, name=f"h_codes{c}", align_bytes=ALIGN)
@@ -193,23 +216,14 @@ def tile_picked_posadd_none_p_kernel(tc, x_words, x_scales, w1, w2, pe, offs, ou
             result = keep.tile([P, OUT_TILES, CHUNK], F32, name=f"result{c}", align_bytes=ALIGN)
             last_banks = [psum.tile([P, CHUNK], F32, name=f"last_bank{a}", tag=f"bank{a}") for a in range(OUT_TILES)]
             second_product(c, grouped, [bank[:] for bank in last_banks])
-            nc.vector.tensor_copy(out=result[:, 0, :], in_=last_banks[0][:])
-            nc.sync.dma_start(out=out_tiles[:, 0, chunks[c]], in_=result[:, 0, :])
-            nc.scalar.copy(out=result[:, 1, :], in_=last_banks[1][:])
-            nc.scalar.dma_start(out=out_tiles[:, 1, chunks[c]], in_=result[:, 1, :])
+            nc.scalar.copy(out=result[:, 0, :], in_=last_banks[0][:])
+            nc.vector.tensor_copy(out=result[:, 1, :], in_=last_banks[1][:])
+            nc.sync.dma_start(out=out_tiles[:, :, chunks[c]], in_=result[:])
 
-        last = CHUNKS - 1
-        grouped = [h_store[:, PACK * S - CHUNK :].bitcast(BF16)]
-        for c in range(1, last):
-            tile = keep.tile([P, CHUNK * PACK], BF16, name=f"h_grouped{c}", tag=f"h_grouped{c}", align_bytes=ALIGN)
-            grouped.append(tile[:])
-        for c in range(last):
-            add_pe(PACK - 1, chunks[c])
-            group_h(c, nc.scalar.copy, grouped[c])
         finish(0, grouped[0])
         add_pe(PACK - 1, chunks[last])
         finish(1, grouped[1])
         last_grouped = keep.tile([P, CHUNK * PACK], BF16, name="h_grouped_last", tag="h_grouped1", align_bytes=ALIGN)
-        group_h(last, nc.vector.tensor_copy, last_grouped[:])
+        group_h(last, nc.vector.tensor_copy, last_grouped[:], every)
         finish(2, grouped[2])
         finish_last(last, last_grouped[:])

@@ -158,7 +158,7 @@ def tile_picked_posadd_none_p_kernel(tc, x_words, x_scales, w1, w2, pe, offs, ou
         chunks = [slice(c * CHUNK, (c + 1) * CHUNK) for c in range(CHUNKS)]
         last = CHUNKS - 1
         grouped = [h_store[:, PACK * S - CHUNK :].bitcast(BF16)]
-        for c in range(1, last):
+        for c in range(1, CHUNKS):
             tile = keep.tile([P, CHUNK * PACK], BF16, name=f"h_grouped{c}", tag=f"h_grouped{c}", align_bytes=ALIGN)
             grouped.append(tile[:])
 
@@ -180,6 +180,8 @@ def tile_picked_posadd_none_p_kernel(tc, x_words, x_scales, w1, w2, pe, offs, ou
             out=w2_grouped[:].rearrange("p (c i j) -> p c j i", i=RUN, j=PACK),
             in_=w2_raw[:].rearrange("p j (c i) -> p c j i", i=RUN),
         )
+
+        group_h(last, nc.scalar.copy, grouped[last], low)
 
         out_tiles = out.rearrange("(a p) s -> p a s", p=P)
         for c in range(last):
@@ -217,13 +219,13 @@ def tile_picked_posadd_none_p_kernel(tc, x_words, x_scales, w1, w2, pe, offs, ou
             last_banks = [psum.tile([P, CHUNK], F32, name=f"last_bank{a}", tag=f"bank{a}") for a in range(OUT_TILES)]
             second_product(c, grouped, [bank[:] for bank in last_banks])
             nc.scalar.copy(out=result[:, 0, :], in_=last_banks[0][:])
+            nc.sync.dma_start(out=out_tiles[:, 0, chunks[c]], in_=result[:, 0, :])
             nc.vector.tensor_copy(out=result[:, 1, :], in_=last_banks[1][:])
-            nc.sync.dma_start(out=out_tiles[:, :, chunks[c]], in_=result[:])
+            nc.sync.dma_start(out=out_tiles[:, 1, chunks[c]], in_=result[:, 1, :])
 
         finish(0, grouped[0])
         add_pe(PACK - 1, chunks[last])
         finish(1, grouped[1])
-        last_grouped = keep.tile([P, CHUNK * PACK], BF16, name="h_grouped_last", tag="h_grouped1", align_bytes=ALIGN)
-        group_h(last, nc.vector.tensor_copy, last_grouped[:], every)
+        group_h(last, nc.vector.tensor_copy, grouped[last], high)
         finish(2, grouped[2])
-        finish_last(last, last_grouped[:])
+        finish_last(last, grouped[last])

@@ -40,7 +40,7 @@ def tile_picked_posadd_none_p_kernel(tc, x_words, x_scales, w1, w2, pe, offs, ou
         w1_raw0 = keep.tile([P, PACK, H], F32, name="w1_raw0", align_bytes=ALIGN)
         w1_raw1 = [keep.tile([P, PAIR, H], F32, name=f"w1_raw1_{u}", align_bytes=ALIGN) for u in range(PACK // PAIR)]
         pe_table = [keep.tile([P, T], F32, name=f"pe_table{t}", align_bytes=ALIGN) for t in range(PACK)]
-        w2_raw = keep.tile([P, PACK, N], F32, name="w2_raw", align_bytes=ALIGN)
+        w2_raw = keep.tile([P, PACK, N], F32, name="w2_raw", tag="w2_raw", align_bytes=ALIGN)
 
         def entries(cols):
             return offsets[:, cols.start // ENTRIES_PER_COLUMN : cols.stop // ENTRIES_PER_COLUMN]
@@ -64,7 +64,7 @@ def tile_picked_posadd_none_p_kernel(tc, x_words, x_scales, w1, w2, pe, offs, ou
             nc.sync.dma_start(out=w1_raw1[u][:], in_=w1_rows[1][:, PAIR * u : PAIR * (u + 1), :])
         load_x(1)
         for t in range(PACK):
-            if t == PACK - 1:
+            if t == PAIR:
                 nc.sync.dma_start(out=w2_raw[:], in_=w2.rearrange("(p j) n -> p j n", j=PACK))
             nc.sync.dma_start(out=pe_table[t][:], in_=pe_planes[t])
 
@@ -101,12 +101,11 @@ def tile_picked_posadd_none_p_kernel(tc, x_words, x_scales, w1, w2, pe, offs, ou
         group_w1(nc.scalar.copy, 1, w1_raw1[1], high, high)
         quantise_w1(1, low)
         quantise_w1(1, high)
-        whole = slice(0, S)
         halves = [slice(0, S // 2), slice(S // 2, S)]
         for part in halves:
             nc.vector.tensor_copy(x_codes[1][:, part], x_table[1][:].bitcast(U32).indirect(entries(part)))
 
-        stretches = [(0, halves[0]), (0, halves[1])] + [(t, whole) for t in range(1, PACK)]
+        stretches = [(t, halves[0]) for t in range(PACK)] + [(t, halves[1]) for t in (1, 0, 2, 3)]
         banks = [
             psum.tile([P, part.stop - part.start], F32, name=f"plane_bank{b}", tag=f"bank{b}")
             for b, (t, part) in enumerate(stretches)
@@ -129,38 +128,28 @@ def tile_picked_posadd_none_p_kernel(tc, x_words, x_scales, w1, w2, pe, offs, ou
             for b in range(len(stretches)):
                 first_product(b, z)
 
-        h_store = keep.tile([P, PACK * S + CHUNK], F32, name="h_store", align_bytes=ALIGN)
-        h = h_store[:, : PACK * S].rearrange("p (t s) -> p t s", t=PACK)
+        h_store = keep.tile([P, PACK * S], F32, name="h_store", align_bytes=ALIGN)
+        h = h_store[:].rearrange("p (t s) -> p t s", t=PACK)
 
-        products = [keep.tile([P, S], F32, name=f"product{t}", tag=f"product{t}", align_bytes=ALIGN) for t in range(PACK - 1)]
-        for b, (t, part) in enumerate(stretches[:-1]):
-            if b != 1:
-                nc.scalar.copy(out=products[t][:, part], in_=banks[b][:])
-        last_products = []
-        for u, part in enumerate(halves):
-            product = keep.tile([P, S // 2], F32, name=f"last_product{u}", tag=f"last_product{u}", align_bytes=ALIGN)
-            nc.scalar.copy(out=product[:], in_=banks[-1][:, part])
-            last_products.append(product)
+        products = {}
+        for b, (t, part) in enumerate(stretches):
+            if (t, part) != (0, halves[1]):
+                name = f"product{t}_{part.start // (S // 2)}"
+                products[t, part.start // (S // 2)] = keep.tile([P, S // 2], F32, name=name, tag=name, align_bytes=ALIGN)
+                nc.scalar.copy(out=products[t, part.start // (S // 2)][:], in_=banks[b][:])
 
         def add_pe(t, part):
-            if t < PACK - 1:
-                product = products[t][:, part]
-            else:
-                u, first = divmod(part.start, S // 2)
-                product = last_products[u][:, first : first + part.stop - part.start]
+            u, first = divmod(part.start, S // 2)
+            product = products[t, u][:, first : first + part.stop - part.start]
             nc.vector.tensor_tensor(h[:, t, part], pe_table[t][:].indirect(entries(part)), product, ADD)
 
-        pe_picked = keep.tile([P, S // 2], F32, name="pe_picked", align_bytes=ALIGN)
+        pe_picked = keep.tile([P, S // 2], F32, name="pe_picked", tag="pe_picked", align_bytes=ALIGN)
         nc.vector.tensor_copy(pe_picked[:], pe_table[0][:].indirect(entries(halves[1])))
         add_pe(0, halves[0])
-        nc.vector.tensor_tensor(h[:, 0, halves[1]], banks[1][:], pe_picked[:], ADD)
+        nc.vector.tensor_tensor(h[:, 0, halves[1]], banks[PACK + 1][:], pe_picked[:], ADD)
 
         chunks = [slice(c * CHUNK, (c + 1) * CHUNK) for c in range(CHUNKS)]
         last = CHUNKS - 1
-        grouped = [h_store[:, PACK * S - CHUNK :].bitcast(BF16)]
-        for c in range(1, CHUNKS):
-            tile = keep.tile([P, CHUNK * PACK], BF16, name=f"h_grouped{c}", tag=f"h_grouped{c}", align_bytes=ALIGN)
-            grouped.append(tile[:])
 
         def group_h(c, copy, target, planes):
             copy(
@@ -168,28 +157,32 @@ def tile_picked_posadd_none_p_kernel(tc, x_words, x_scales, w1, w2, pe, offs, ou
                 in_=h[:, planes, chunks[c]].rearrange("p t (c i) -> p c t i", i=RUN),
             )
 
-        every = slice(0, PACK)
-        add_pe(1, halves[0])
-        for c in range(CHUNKS // 2):
-            group_h(c, nc.scalar.copy, grouped[c], low)
-        add_pe(1, halves[1])
-        add_pe(2, whole)
-
-        w2_grouped = keep.tile([P, N * PACK], BF16, name="w2_grouped", tag="product1", align_bytes=ALIGN)
+        w2_grouped = keep.tile([P, N * PACK], BF16, name="w2_grouped", tag="pe_picked", align_bytes=ALIGN)
         nc.scalar.copy(
             out=w2_grouped[:].rearrange("p (c i j) -> p c j i", i=RUN, j=PACK),
             in_=w2_raw[:].rearrange("p j (c i) -> p c j i", i=RUN),
         )
 
+        h_grouped = keep.tile([P, S * PACK], BF16, name="h_grouped", tag="w2_raw", align_bytes=ALIGN)
+        grouped = [h_grouped[:, part.start * PACK : part.stop * PACK] for part in chunks]
+
+        add_pe(1, halves[0])
+        for c in range(CHUNKS // 2):
+            group_h(c, nc.scalar.copy, grouped[c], low)
+        add_pe(1, halves[1])
         group_h(last, nc.scalar.copy, grouped[last], low)
+        add_pe(2, halves[0])
+        group_h(2, nc.vector.tensor_copy, grouped[2], low)
+        add_pe(2, halves[1])
 
         out_tiles = out.rearrange("(a p) s -> p a s", p=P)
-        for c in range(last):
+        for c in range(CHUNKS):
             add_pe(PACK - 1, chunks[c])
-            group_h(c, nc.scalar.copy, grouped[c], high if c < CHUNKS // 2 else every)
-        w2_codes = keep.tile([P, N], U32, name="w2_codes", tag="last_product0", align_bytes=ALIGN)
-        w2_scales = keep.tile([P, N], U8, name="w2_scales", align_bytes=ALIGN)
-        nc.vector.quantize_mx(out=w2_codes[:].bitcast(FP8X4), scales=w2_scales[:], in_=w2_grouped[:])
+            group_h(c, nc.scalar.copy, grouped[c], high)
+            if c == last - 1:
+                w2_codes = keep.tile([P, N], U32, name="w2_codes", tag="product3_0", align_bytes=ALIGN)
+                w2_scales = keep.tile([P, N], U8, name="w2_scales", align_bytes=ALIGN)
+                nc.vector.quantize_mx(out=w2_codes[:].bitcast(FP8X4), scales=w2_scales[:], in_=w2_grouped[:])
 
         def second_product(c, grouped, sums):
             codes = keep.tile([P, CHUNK], U32, name=f"h_codes{c}", align_bytes=ALIGN)
@@ -207,25 +200,19 @@ def tile_picked_posadd_none_p_kernel(tc, x_words, x_scales, w1, w2, pe, offs, ou
                     stop=True,
                 )
 
-        def finish(c, grouped):
-            result = keep.tile([P, OUT_TILES, CHUNK], F32, name=f"result{c}", align_bytes=ALIGN)
-            bank = psum.tile([P, OUT_TILES, CHUNK], F32, name=f"out_bank{c}")
-            second_product(c, grouped, [bank[:, a, :] for a in range(OUT_TILES)])
-            nc.scalar.copy(out=result[:], in_=bank[:])
-            nc.sync.dma_start(out=out_tiles[:, :, chunks[c]], in_=result[:])
-
-        def finish_last(c, grouped):
-            result = keep.tile([P, OUT_TILES, CHUNK], F32, name=f"result{c}", align_bytes=ALIGN)
-            last_banks = [psum.tile([P, CHUNK], F32, name=f"last_bank{a}", tag=f"bank{a}") for a in range(OUT_TILES)]
-            second_product(c, grouped, [bank[:] for bank in last_banks])
-            nc.scalar.copy(out=result[:, 0, :], in_=last_banks[0][:])
-            nc.sync.dma_start(out=out_tiles[:, 0, chunks[c]], in_=result[:, 0, :])
-            nc.vector.tensor_copy(out=result[:, 1, :], in_=last_banks[1][:])
-            nc.sync.dma_start(out=out_tiles[:, 1, chunks[c]], in_=result[:, 1, :])
-
-        finish(0, grouped[0])
-        add_pe(PACK - 1, chunks[last])
-        finish(1, grouped[1])
-        group_h(last, nc.vector.tensor_copy, grouped[last], high)
-        finish(2, grouped[2])
-        finish_last(last, grouped[last])
+        results = [keep.tile([P, OUT_TILES, CHUNK], F32, name=f"result{c}", align_bytes=ALIGN) for c in range(CHUNKS)]
+        sums = []
+        for c in range(last):
+            bank = psum.tile([P, OUT_TILES, CHUNK], F32, name=f"out_bank{c}", tag=f"bank{OUT_TILES + c}")
+            second_product(c, grouped[c], [bank[:, a, :] for a in range(OUT_TILES)])
+            sums.append(bank)
+        last_banks = [psum.tile([P, CHUNK], F32, name=f"last_bank{a}", tag=f"bank{a}") for a in range(OUT_TILES)]
+        second_product(last, grouped[last], [bank[:] for bank in last_banks])
+        for c in range(last):
+            copy = nc.vector.tensor_copy if c == 1 else nc.scalar.copy
+            copy(out=results[c][:], in_=sums[c][:])
+            nc.sync.dma_start(out=out_tiles[:, :, chunks[c]], in_=results[c][:])
+        nc.vector.tensor_copy(out=results[last][:, 1, :], in_=last_banks[1][:])
+        nc.sync.dma_start(out=out_tiles[:, 1, chunks[last]], in_=results[last][:, 1, :])
+        nc.scalar.copy(out=results[last][:, 0, :], in_=last_banks[0][:])
+        nc.sync.dma_start(out=out_tiles[:, 0, chunks[last]], in_=results[last][:, 0, :])

@@ -105,7 +105,7 @@ def tile_picked_posadd_none_p_kernel(tc, x_words, x_scales, w1, w2, pe, offs, ou
         for part in halves:
             nc.vector.tensor_copy(x_codes[1][:, part], x_table[1][:].bitcast(U32).indirect(entries(part)))
 
-        stretches = [(t, halves[0]) for t in range(PACK)] + [(t, halves[1]) for t in (1, 0, 2, 3)]
+        stretches = [(t, part) for pair in (low, high) for part in halves for t in range(pair.start, pair.stop)]
         banks = [
             psum.tile([P, part.stop - part.start], F32, name=f"plane_bank{b}", tag=f"bank{b}")
             for b, (t, part) in enumerate(stretches)
@@ -146,7 +146,7 @@ def tile_picked_posadd_none_p_kernel(tc, x_words, x_scales, w1, w2, pe, offs, ou
         pe_picked = keep.tile([P, S // 2], F32, name="pe_picked", tag="pe_picked", align_bytes=ALIGN)
         nc.vector.tensor_copy(pe_picked[:], pe_table[0][:].indirect(entries(halves[1])))
         add_pe(0, halves[0])
-        nc.vector.tensor_tensor(h[:, 0, halves[1]], banks[PACK + 1][:], pe_picked[:], ADD)
+        nc.vector.tensor_tensor(h[:, 0, halves[1]], banks[PAIR][:], pe_picked[:], ADD)
 
         chunks = [slice(c * CHUNK, (c + 1) * CHUNK) for c in range(CHUNKS)]
         last = CHUNKS - 1

@@ -64,7 +64,7 @@ def tile_picked_posadd_none_p_kernel(tc, x_words, x_scales, w1, w2, pe, offs, ou
             nc.sync.dma_start(out=w1_raw1[u][:], in_=w1_rows[1][:, PAIR * u : PAIR * (u + 1), :])
         load_x(1)
         for t in range(PACK):
-            if t == PAIR:
+            if t == PACK - 1:
                 nc.sync.dma_start(out=w2_raw[:], in_=w2.rearrange("(p j) n -> p j n", j=PACK))
             nc.sync.dma_start(out=pe_table[t][:], in_=pe_planes[t])
 
@@ -128,8 +128,7 @@ def tile_picked_posadd_none_p_kernel(tc, x_words, x_scales, w1, w2, pe, offs, ou
             for b in range(len(stretches)):
                 first_product(b, z)
 
-        h_store = keep.tile([P, PACK * S], F32, name="h_store", align_bytes=ALIGN)
-        h = h_store[:].rearrange("p (t s) -> p t s", t=PACK)
+        h = keep.tile([P, PACK, S], F32, name="h", align_bytes=ALIGN)
 
         products = {}
         for b, (t, part) in enumerate(stretches):
@@ -151,65 +150,74 @@ def tile_picked_posadd_none_p_kernel(tc, x_words, x_scales, w1, w2, pe, offs, ou
         chunks = [slice(c * CHUNK, (c + 1) * CHUNK) for c in range(CHUNKS)]
         last = CHUNKS - 1
 
-        def group_h(c, copy, target, planes):
+        grouped = []
+        for c in range(CHUNKS):
+            tile = keep.tile([P, CHUNK * PACK], BF16, name=f"h_grouped{c}", tag=f"h_grouped{c}", align_bytes=ALIGN)
+            grouped.append(tile[:])
+
+        def group_h(copy, c, planes):
             copy(
-                out=target.rearrange("p (c i t) -> p c t i", i=RUN, t=PACK)[:, :, planes, :],
+                out=grouped[c].rearrange("p (c i t) -> p c t i", i=RUN, t=PACK)[:, :, planes, :],
                 in_=h[:, planes, chunks[c]].rearrange("p t (c i) -> p c t i", i=RUN),
             )
 
-        w2_grouped = keep.tile([P, N * PACK], BF16, name="w2_grouped", tag="pe_picked", align_bytes=ALIGN)
+        for c in range(2):
+            add_pe(1, chunks[c])
+            group_h(nc.scalar.copy, c, low)
+        add_pe(1, halves[1])
+        group_h(nc.scalar.copy, 2, low)
+
+        w2_grouped = keep.tile([P, N * PACK], BF16, name="w2_grouped", tag="product1_0", align_bytes=ALIGN)
         nc.scalar.copy(
             out=w2_grouped[:].rearrange("p (c i j) -> p c j i", i=RUN, j=PACK),
             in_=w2_raw[:].rearrange("p j (c i) -> p c j i", i=RUN),
         )
 
-        h_grouped = keep.tile([P, S * PACK], BF16, name="h_grouped", tag="w2_raw", align_bytes=ALIGN)
-        grouped = [h_grouped[:, part.start * PACK : part.stop * PACK] for part in chunks]
-
-        add_pe(1, halves[0])
-        for c in range(CHUNKS // 2):
-            group_h(c, nc.scalar.copy, grouped[c], low)
-        add_pe(1, halves[1])
-        group_h(last, nc.scalar.copy, grouped[last], low)
-        add_pe(2, halves[0])
-        group_h(2, nc.vector.tensor_copy, grouped[2], low)
-        add_pe(2, halves[1])
+        for part in halves:
+            add_pe(2, part)
 
         out_tiles = out.rearrange("(a p) s -> p a s", p=P)
+        h_codes = [keep.tile([P, CHUNK], U32, name=f"h_codes{c}", align_bytes=ALIGN) for c in range(CHUNKS)]
+        h_scales = [keep.tile([P, CHUNK], U8, name=f"h_scales{c}", align_bytes=ALIGN) for c in range(CHUNKS)]
+
+        def quantise_h(c):
+            nc.vector.quantize_mx(out=h_codes[c][:].bitcast(FP8X4), scales=h_scales[c][:], in_=grouped[c])
+
         for c in range(CHUNKS):
             add_pe(PACK - 1, chunks[c])
-            group_h(c, nc.scalar.copy, grouped[c], high)
-            if c == last - 1:
-                w2_codes = keep.tile([P, N], U32, name="w2_codes", tag="product3_0", align_bytes=ALIGN)
-                w2_scales = keep.tile([P, N], U8, name="w2_scales", align_bytes=ALIGN)
-                nc.vector.quantize_mx(out=w2_codes[:].bitcast(FP8X4), scales=w2_scales[:], in_=w2_grouped[:])
+            group_h(nc.scalar.copy, c, high if c < last else slice(0, PACK))
+        w2_codes = keep.tile([P, N], U32, name="w2_codes", tag="product3_0", align_bytes=ALIGN)
+        w2_scales = keep.tile([P, N], U8, name="w2_scales", align_bytes=ALIGN)
+        nc.vector.quantize_mx(out=w2_codes[:].bitcast(FP8X4), scales=w2_scales[:], in_=w2_grouped[:])
+        for c in range(CHUNKS):
+            quantise_h(c)
 
-        def second_product(c, grouped, sums):
-            codes = keep.tile([P, CHUNK], U32, name=f"h_codes{c}", align_bytes=ALIGN)
-            scales = keep.tile([P, CHUNK], U8, name=f"h_scales{c}", align_bytes=ALIGN)
-            nc.vector.quantize_mx(out=codes[:].bitcast(FP8X4), scales=scales[:], in_=grouped)
+        def second_product(c, sums):
             for a in range(OUT_TILES):
                 cols = slice(a * P, (a + 1) * P)
                 nc.tensor.matmul_mx(
                     out=sums[a],
                     lhsT=w2_codes[:, cols].bitcast(FP8X4),
                     lhsT_scale=w2_scales[:, cols],
-                    rhs=codes[:].bitcast(FP8X4),
-                    rhs_scale=scales[:],
+                    rhs=h_codes[c][:].bitcast(FP8X4),
+                    rhs_scale=h_scales[c][:],
                     start=True,
                     stop=True,
                 )
 
-        results = [keep.tile([P, OUT_TILES, CHUNK], F32, name=f"result{c}", align_bytes=ALIGN) for c in range(CHUNKS)]
+        results = [
+            keep.tile([P, OUT_TILES, CHUNK], F32, name=f"result{c}", tag=f"h_grouped{last}" if c == 2 else f"result{c}", align_bytes=ALIGN)
+            for c in range(CHUNKS)
+        ]
         sums = []
         for c in range(last):
             bank = psum.tile([P, OUT_TILES, CHUNK], F32, name=f"out_bank{c}", tag=f"bank{OUT_TILES + c}")
-            second_product(c, grouped[c], [bank[:, a, :] for a in range(OUT_TILES)])
+            second_product(c, [bank[:, a, :] for a in range(OUT_TILES)])
             sums.append(bank)
         last_banks = [psum.tile([P, CHUNK], F32, name=f"last_bank{a}", tag=f"bank{a}") for a in range(OUT_TILES)]
-        second_product(last, grouped[last], [bank[:] for bank in last_banks])
+        second_product(last, [bank[:] for bank in last_banks])
         for c in range(last):
-            copy = nc.vector.tensor_copy if c == 1 else nc.scalar.copy
+            copy = nc.vector.tensor_copy if c == 2 else nc.scalar.copy
             copy(out=results[c][:], in_=sums[c][:])
             nc.sync.dma_start(out=out_tiles[:, :, chunks[c]], in_=results[c][:])
         nc.vector.tensor_copy(out=results[last][:, 1, :], in_=last_banks[1][:])

@@ -105,7 +105,8 @@ def tile_picked_posadd_none_p_kernel(tc, x_words, x_scales, w1, w2, pe, offs, ou
         for part in halves:
             nc.vector.tensor_copy(x_codes[1][:, part], x_table[1][:].bitcast(U32).indirect(entries(part)))
 
-        stretches = [(t, part) for pair in (low, high) for part in halves for t in range(pair.start, pair.stop)]
+        whole = slice(0, S)
+        stretches = [(t, part) for part in halves for t in range(PAIR)] + [(2, whole)] + [(3, part) for part in halves]
         banks = [
             psum.tile([P, part.stop - part.start], F32, name=f"plane_bank{b}", tag=f"bank{b}")
             for b, (t, part) in enumerate(stretches)
@@ -134,13 +135,13 @@ def tile_picked_posadd_none_p_kernel(tc, x_words, x_scales, w1, w2, pe, offs, ou
         for b, (t, part) in enumerate(stretches):
             if (t, part) != (0, halves[1]):
                 name = f"product{t}_{part.start // (S // 2)}"
-                products[t, part.start // (S // 2)] = keep.tile([P, S // 2], F32, name=name, tag=name, align_bytes=ALIGN)
-                nc.scalar.copy(out=products[t, part.start // (S // 2)][:], in_=banks[b][:])
+                products[t, part.start] = keep.tile([P, part.stop - part.start], F32, name=name, tag=name, align_bytes=ALIGN)
+                nc.scalar.copy(out=products[t, part.start][:], in_=banks[b][:])
 
-        def add_pe(t, part):
-            u, first = divmod(part.start, S // 2)
-            product = products[t, u][:, first : first + part.stop - part.start]
-            nc.vector.tensor_tensor(h[:, t, part], pe_table[t][:].indirect(entries(part)), product, ADD)
+        def add_pe(t, part, place=None):
+            first = max(start for plane, start in products if plane == t and start <= part.start)
+            product = products[t, first][:, part.start - first : part.stop - first]
+            nc.vector.tensor_tensor(h[:, t, place or part], pe_table[t][:].indirect(entries(part)), product, ADD)
 
         pe_picked = keep.tile([P, S // 2], F32, name="pe_picked", tag="pe_picked", align_bytes=ALIGN)
         nc.vector.tensor_copy(pe_picked[:], pe_table[0][:].indirect(entries(halves[1])))
@@ -155,10 +156,10 @@ def tile_picked_posadd_none_p_kernel(tc, x_words, x_scales, w1, w2, pe, offs, ou
             tile = keep.tile([P, CHUNK * PACK], BF16, name=f"h_grouped{c}", tag=f"h_grouped{c}", align_bytes=ALIGN)
             grouped.append(tile[:])
 
-        def group_h(copy, c, planes):
+        def group_h(copy, c, planes, src=None):
             copy(
                 out=grouped[c].rearrange("p (c i t) -> p c t i", i=RUN, t=PACK)[:, :, planes, :],
-                in_=h[:, planes, chunks[c]].rearrange("p t (c i) -> p c t i", i=RUN),
+                in_=(h[:, planes, chunks[c]] if src is None else src).rearrange("p t (c i) -> p c t i", i=RUN),
             )
 
         for c in range(2):
@@ -173,8 +174,7 @@ def tile_picked_posadd_none_p_kernel(tc, x_words, x_scales, w1, w2, pe, offs, ou
             in_=w2_raw[:].rearrange("p j (c i) -> p c j i", i=RUN),
         )
 
-        for part in halves:
-            add_pe(2, part)
+        add_pe(2, whole)
 
         out_tiles = out.rearrange("(a p) s -> p a s", p=P)
         h_codes = [keep.tile([P, CHUNK], U32, name=f"h_codes{c}", align_bytes=ALIGN) for c in range(CHUNKS)]
@@ -183,13 +183,19 @@ def tile_picked_posadd_none_p_kernel(tc, x_words, x_scales, w1, w2, pe, offs, ou
         def quantise_h(c):
             nc.vector.quantize_mx(out=h_codes[c][:].bitcast(FP8X4), scales=h_scales[c][:], in_=grouped[c])
 
-        for c in range(CHUNKS):
+        add_pe(PACK - 1, chunks[0], chunks[last])
+        blocks = h[:].rearrange("p t (c s) -> p (t c) s", s=CHUNK)
+        group_h(nc.scalar.copy, 0, high, blocks[:, PAIR * CHUNKS :: PAIR * CHUNKS - 1, :])
+        for c in range(1, last):
             add_pe(PACK - 1, chunks[c])
-            group_h(nc.scalar.copy, c, high if c < last else slice(0, PACK))
+            group_h(nc.scalar.copy, c, high)
         w2_codes = keep.tile([P, N], U32, name="w2_codes", tag="product3_0", align_bytes=ALIGN)
         w2_scales = keep.tile([P, N], U8, name="w2_scales", align_bytes=ALIGN)
         nc.vector.quantize_mx(out=w2_codes[:].bitcast(FP8X4), scales=w2_scales[:], in_=w2_grouped[:])
-        for c in range(CHUNKS):
+        quantise_h(0)
+        add_pe(PACK - 1, chunks[last])
+        group_h(nc.scalar.copy, last, every)
+        for c in range(1, CHUNKS):
             quantise_h(c)
 
         def second_product(c, sums):
@@ -217,7 +223,7 @@ def tile_picked_posadd_none_p_kernel(tc, x_words, x_scales, w1, w2, pe, offs, ou
         last_banks = [psum.tile([P, CHUNK], F32, name=f"last_bank{a}", tag=f"bank{a}") for a in range(OUT_TILES)]
         second_product(last, [bank[:] for bank in last_banks])
         for c in range(last):
-            copy = nc.vector.tensor_copy if c == 2 else nc.scalar.copy
+            copy = nc.vector.tensor_copy if c != 1 else nc.scalar.copy
             copy(out=results[c][:], in_=sums[c][:])
             nc.sync.dma_start(out=out_tiles[:, :, chunks[c]], in_=results[c][:])
         nc.vector.tensor_copy(out=results[last][:, 1, :], in_=last_banks[1][:])

@@ -13,6 +13,7 @@ U16 = mybir.dt.uint16
 U8 = mybir.dt.uint8
 FP8X4 = mybir.dt.float8_e4m3fn_x4
 ADD = mybir.AluOpType.add
+COPY = mybir.ActivationFunctionType.Copy
 
 P = 128
 PACK = 4
@@ -24,6 +25,7 @@ ENTRIES_PER_COLUMN = 16
 RUN = 4
 CHUNK = 128
 CHUNKS = S // CHUNK
+HALF = S // 2
 OUT_TILES = N // P
 ALIGN = 64
 
@@ -37,10 +39,9 @@ def tile_picked_posadd_none_p_kernel(tc, x_words, x_scales, w1, w2, pe, offs, ou
         offsets = keep.tile([P, S // ENTRIES_PER_COLUMN], U16, name="offsets")
         x_table = [keep.tile([P, T], I32, name=f"x_table{z}", align_bytes=ALIGN) for z in range(PASSES)]
         scale_table = keep.tile([P, T], U8, name="scale_table", align_bytes=ALIGN)
-        w1_raw0 = keep.tile([P, PACK, H], F32, name="w1_raw0", align_bytes=ALIGN)
-        w1_raw1 = [keep.tile([P, PAIR, H], F32, name=f"w1_raw1_{u}", align_bytes=ALIGN) for u in range(PACK // PAIR)]
+        w1_raw = [keep.tile([P, PACK, H], F32, name=f"w1_raw{z}", align_bytes=ALIGN) for z in range(PASSES)]
         pe_table = [keep.tile([P, T], F32, name=f"pe_table{t}", align_bytes=ALIGN) for t in range(PACK)]
-        w2_raw = keep.tile([P, PACK, N], F32, name="w2_raw", tag="w2_raw", align_bytes=ALIGN)
+        w2_raw = keep.tile([P, PACK, N], F32, name="w2_raw", align_bytes=ALIGN)
 
         def entries(cols):
             return offsets[:, cols.start // ENTRIES_PER_COLUMN : cols.stop // ENTRIES_PER_COLUMN]
@@ -59,174 +60,141 @@ def tile_picked_posadd_none_p_kernel(tc, x_words, x_scales, w1, w2, pe, offs, ou
                 out=scale_table[QUADRANT * q : QUADRANT * q + SCALE_ROWS * PASSES, :].bitcast(I32),
                 in_=x_scales[:, SCALE_ROWS * q : SCALE_ROWS * (q + 1), :].bitcast(I32),
             )
-        nc.sync.dma_start(out=w1_raw0[:], in_=w1_rows[0])
-        for u in range(PACK // PAIR):
-            nc.sync.dma_start(out=w1_raw1[u][:], in_=w1_rows[1][:, PAIR * u : PAIR * (u + 1), :])
+        for z in range(PASSES):
+            nc.sync.dma_start(out=w1_raw[z][:], in_=w1_rows[z])
         load_x(1)
         for t in range(PACK):
             if t == PACK - 1:
                 nc.sync.dma_start(out=w2_raw[:], in_=w2.rearrange("(p j) n -> p j n", j=PACK))
             nc.sync.dma_start(out=pe_table[t][:], in_=pe_planes[t])
 
+        pairs = [slice(0, PAIR), slice(PAIR, PACK)]
+        halves = [slice(0, HALF), slice(HALF, S)]
+        chunks = [slice(c * CHUNK, (c + 1) * CHUNK) for c in range(CHUNKS)]
         w1_codes = [keep.tile([P, H], U32, name=f"w1_codes{z}", align_bytes=ALIGN) for z in range(PASSES)]
         w1_scales = [keep.tile([P, H], U8, name=f"w1_scales{z}", align_bytes=ALIGN) for z in range(PASSES)]
-        w1_grouped = [keep.tile([P, PACK, P, PACK], BF16, name=f"w1_grouped{z}", tag=f"w1_grouped{z}", align_bytes=ALIGN) for z in range(PASSES)]
+        w1_grouped = [
+            [keep.tile([P, PAIR, P, PACK], BF16, name=f"w1_grouped{z}_{u}", align_bytes=ALIGN) for u in range(len(pairs))]
+            for z in range(PASSES)
+        ]
 
-        def group_w1(copy, z, raw, rows, planes):
-            dst = w1_grouped[z][:].rearrange("p t m j -> p m j t")
-            src = raw[:].rearrange("p j (m t) -> p m j t", t=PACK)
-            copy(out=dst[:, :, rows, planes], in_=src[:, :, :, planes])
+        def group_w1(copy, z, u):
+            src = w1_raw[z][:].rearrange("p j (m t) -> p m j t", t=PACK)
+            copy(out=w1_grouped[z][u][:].rearrange("p t m j -> p m j t"), in_=src[:, :, :, pairs[u]])
 
-        def quantise_w1(z, planes):
-            cols = slice(planes.start * P, planes.stop * P)
+        def quantise_w1(z, u):
+            cols = slice(pairs[u].start * P, pairs[u].stop * P)
             nc.vector.quantize_mx(
                 out=w1_codes[z][:, cols].bitcast(FP8X4),
                 scales=w1_scales[z][:, cols],
-                in_=w1_grouped[z][:, planes].rearrange("p t m j -> p (t m j)"),
+                in_=w1_grouped[z][u][:].rearrange("p t m j -> p (t m j)"),
             )
 
         x_codes = [keep.tile([P, S], U32, name=f"x_codes{z}", align_bytes=ALIGN) for z in range(PASSES)]
         x_picked_scales = keep.tile([P, S], U8, name="x_picked_scales", align_bytes=ALIGN)
         nc.vector.tensor_copy(x_codes[0][:], x_table[0][:].bitcast(U32).indirect(offsets[:]))
         nc.vector.tensor_copy(x_picked_scales[:], scale_table[:].indirect(offsets[:]))
-
-        low, high, every = slice(0, PAIR), slice(PAIR, PACK), slice(0, PACK)
-        group_w1(nc.vector.tensor_copy, 0, w1_raw0, every, low)
-        group_w1(nc.scalar.copy, 0, w1_raw0, every, high)
-        quantise_w1(0, low)
-        group_w1(nc.scalar.copy, 1, w1_raw1[0], low, low)
-        group_w1(nc.vector.tensor_copy, 1, w1_raw1[0], low, high)
-        quantise_w1(0, high)
-        group_w1(nc.vector.tensor_copy, 1, w1_raw1[1], high, low)
-        group_w1(nc.scalar.copy, 1, w1_raw1[1], high, high)
-        quantise_w1(1, low)
-        quantise_w1(1, high)
-        halves = [slice(0, S // 2), slice(S // 2, S)]
+        for z in range(PASSES):
+            group_w1(nc.vector.tensor_copy, z, 0)
+            group_w1(nc.scalar.copy, z, 1)
+            for u in range(len(pairs)):
+                quantise_w1(z, u)
         for part in halves:
             nc.vector.tensor_copy(x_codes[1][:, part], x_table[1][:].bitcast(U32).indirect(entries(part)))
 
-        whole = slice(0, S)
-        stretches = [(t, part) for part in halves for t in range(PAIR)] + [(2, whole)] + [(3, part) for part in halves]
-        banks = [
-            psum.tile([P, part.stop - part.start], F32, name=f"plane_bank{b}", tag=f"bank{b}")
-            for b, (t, part) in enumerate(stretches)
-        ]
+        banks = {}
 
-        def first_product(b, z):
-            t, part = stretches[b]
-            cols = slice(t * P, (t + 1) * P)
-            nc.tensor.matmul_mx(
-                out=banks[b][:],
-                lhsT=w1_codes[z][:, cols].bitcast(FP8X4),
-                lhsT_scale=w1_scales[z][:, cols],
-                rhs=x_codes[z][:, part].bitcast(FP8X4),
-                rhs_scale=x_picked_scales[SCALE_ROWS * z :, part],
-                start=(z == 0),
-                stop=(z == PASSES - 1),
+        def first_product(u, g):
+            banks[u, g] = psum.tile([P, PAIR, HALF], F32, name=f"plane_bank{u}_{g}", tag=f"bank{g}")
+            for z in range(PASSES):
+                for e in range(PAIR):
+                    cols = slice((PAIR * u + e) * P, (PAIR * u + e + 1) * P)
+                    nc.tensor.matmul_mx(
+                        out=banks[u, g][:, e, :],
+                        lhsT=w1_codes[z][:, cols].bitcast(FP8X4),
+                        lhsT_scale=w1_scales[z][:, cols],
+                        rhs=x_codes[z][:, halves[g]].bitcast(FP8X4),
+                        rhs_scale=x_picked_scales[SCALE_ROWS * z :, halves[g]],
+                        start=(z == 0 and e == 0),
+                        stop=(z == PASSES - 1 and e == PAIR - 1),
+                    )
+
+        for g in range(len(halves)):
+            first_product(0, g)
+
+        pe_picked = [keep.tile([P, PAIR, S], F32, name=f"pe_picked{u}", align_bytes=ALIGN) for u in range(len(pairs))]
+        h_grouped = [keep.tile([P, CHUNK * PACK], BF16, name=f"h_grouped{c}", align_bytes=ALIGN) for c in range(CHUNKS)]
+
+        def pick_pe(t, part):
+            nc.scalar.activation(pe_picked[t // PAIR][:, t % PAIR, part], pe_table[t][:].indirect(entries(part)), COPY)
+
+        def add_pe(u, c):
+            g, first = divmod(c * CHUNK, HALF)
+            walk = "p t (c i) -> p c t i"
+            nc.vector.tensor_tensor(
+                h_grouped[c][:].rearrange("p (c i t) -> p c t i", i=RUN, t=PACK)[:, :, pairs[u], :],
+                banks[u, g][:, :, first : first + CHUNK].rearrange(walk, i=RUN),
+                pe_picked[u][:, :, chunks[c]].rearrange(walk, i=RUN),
+                ADD,
             )
 
-        for z in range(PASSES):
-            for b in range(len(stretches)):
-                first_product(b, z)
-
-        h = keep.tile([P, PACK, S], F32, name="h", align_bytes=ALIGN)
-
-        products = {}
-        for b, (t, part) in enumerate(stretches):
-            if (t, part) != (0, halves[1]):
-                name = f"product{t}_{part.start // (S // 2)}"
-                products[t, part.start] = keep.tile([P, part.stop - part.start], F32, name=name, tag=name, align_bytes=ALIGN)
-                nc.scalar.copy(out=products[t, part.start][:], in_=banks[b][:])
-
-        def add_pe(t, part, place=None):
-            first = max(start for plane, start in products if plane == t and start <= part.start)
-            product = products[t, first][:, part.start - first : part.stop - first]
-            nc.vector.tensor_tensor(h[:, t, place or part], pe_table[t][:].indirect(entries(part)), product, ADD)
-
-        pe_picked = keep.tile([P, S // 2], F32, name="pe_picked", tag="pe_picked", align_bytes=ALIGN)
-        nc.vector.tensor_copy(pe_picked[:], pe_table[0][:].indirect(entries(halves[1])))
-        add_pe(0, halves[0])
-        nc.vector.tensor_tensor(h[:, 0, halves[1]], banks[PAIR][:], pe_picked[:], ADD)
-
-        chunks = [slice(c * CHUNK, (c + 1) * CHUNK) for c in range(CHUNKS)]
-        last = CHUNKS - 1
-
-        grouped = []
+        pick_pe(0, slice(0, S))
+        for part in halves:
+            pick_pe(1, part)
         for c in range(CHUNKS):
-            tile = keep.tile([P, CHUNK * PACK], BF16, name=f"h_grouped{c}", tag=f"h_grouped{c}", align_bytes=ALIGN)
-            grouped.append(tile[:])
+            add_pe(0, c)
+        for g in range(len(halves)):
+            first_product(1, g)
+        pick_pe(2, slice(0, S))
 
-        def group_h(copy, c, planes, src=None):
+        w2_grouped = [keep.tile([P, P * PACK], BF16, name=f"w2_grouped{a}", align_bytes=ALIGN) for a in range(OUT_TILES)]
+        w2_codes = [keep.tile([P, P], U32, name=f"w2_codes{a}", align_bytes=ALIGN) for a in range(OUT_TILES)]
+        w2_scales = [keep.tile([P, P], U8, name=f"w2_scales{a}", align_bytes=ALIGN) for a in range(OUT_TILES)]
+        for a, copy in enumerate((nc.vector.tensor_copy, nc.scalar.copy)):
             copy(
-                out=grouped[c].rearrange("p (c i t) -> p c t i", i=RUN, t=PACK)[:, :, planes, :],
-                in_=(h[:, planes, chunks[c]] if src is None else src).rearrange("p t (c i) -> p c t i", i=RUN),
+                out=w2_grouped[a][:].rearrange("p (c i j) -> p c j i", i=RUN, j=PACK),
+                in_=w2_raw[:, :, a * P : (a + 1) * P].rearrange("p j (c i) -> p c j i", i=RUN),
             )
-
-        for c in range(2):
-            add_pe(1, chunks[c])
-            group_h(nc.scalar.copy, c, low)
-        add_pe(1, halves[1])
-        group_h(nc.scalar.copy, 2, low)
-
-        w2_grouped = keep.tile([P, N * PACK], BF16, name="w2_grouped", tag="product1_0", align_bytes=ALIGN)
-        nc.scalar.copy(
-            out=w2_grouped[:].rearrange("p (c i j) -> p c j i", i=RUN, j=PACK),
-            in_=w2_raw[:].rearrange("p j (c i) -> p c j i", i=RUN),
-        )
-
-        add_pe(2, whole)
+        for a in range(OUT_TILES):
+            nc.vector.quantize_mx(out=w2_codes[a][:].bitcast(FP8X4), scales=w2_scales[a][:], in_=w2_grouped[a][:])
 
         out_tiles = out.rearrange("(a p) s -> p a s", p=P)
         h_codes = [keep.tile([P, CHUNK], U32, name=f"h_codes{c}", align_bytes=ALIGN) for c in range(CHUNKS)]
         h_scales = [keep.tile([P, CHUNK], U8, name=f"h_scales{c}", align_bytes=ALIGN) for c in range(CHUNKS)]
 
         def quantise_h(c):
-            nc.vector.quantize_mx(out=h_codes[c][:].bitcast(FP8X4), scales=h_scales[c][:], in_=grouped[c])
+            nc.vector.quantize_mx(out=h_codes[c][:].bitcast(FP8X4), scales=h_scales[c][:], in_=h_grouped[c][:])
 
-        add_pe(PACK - 1, chunks[0], chunks[last])
-        blocks = h[:].rearrange("p t (c s) -> p (t c) s", s=CHUNK)
-        group_h(nc.scalar.copy, 0, high, blocks[:, PAIR * CHUNKS :: PAIR * CHUNKS - 1, :])
-        for c in range(1, last):
-            add_pe(PACK - 1, chunks[c])
-            group_h(nc.scalar.copy, c, high)
-        w2_codes = keep.tile([P, N], U32, name="w2_codes", tag="product3_0", align_bytes=ALIGN)
-        w2_scales = keep.tile([P, N], U8, name="w2_scales", align_bytes=ALIGN)
-        nc.vector.quantize_mx(out=w2_codes[:].bitcast(FP8X4), scales=w2_scales[:], in_=w2_grouped[:])
-        quantise_h(0)
-        add_pe(PACK - 1, chunks[last])
-        group_h(nc.scalar.copy, last, every)
-        for c in range(1, CHUNKS):
-            quantise_h(c)
+        for c in range(CHUNKS):
+            pick_pe(PACK - 1, chunks[c])
+        for c in range(CHUNKS):
+            add_pe(1, c)
+            if c > 0:
+                quantise_h(c - 1)
+        quantise_h(CHUNKS - 1)
 
         def second_product(c, sums):
             for a in range(OUT_TILES):
-                cols = slice(a * P, (a + 1) * P)
                 nc.tensor.matmul_mx(
                     out=sums[a],
-                    lhsT=w2_codes[:, cols].bitcast(FP8X4),
-                    lhsT_scale=w2_scales[:, cols],
+                    lhsT=w2_codes[a][:].bitcast(FP8X4),
+                    lhsT_scale=w2_scales[a][:],
                     rhs=h_codes[c][:].bitcast(FP8X4),
                     rhs_scale=h_scales[c][:],
                     start=True,
                     stop=True,
                 )
 
-        results = [
-            keep.tile([P, OUT_TILES, CHUNK], F32, name=f"result{c}", tag=f"h_grouped{last}" if c == 2 else f"result{c}", align_bytes=ALIGN)
-            for c in range(CHUNKS)
-        ]
-        sums = []
+        last = CHUNKS - 1
         for c in range(last):
-            bank = psum.tile([P, OUT_TILES, CHUNK], F32, name=f"out_bank{c}", tag=f"bank{OUT_TILES + c}")
+            bank = psum.tile([P, OUT_TILES, CHUNK], F32, name=f"out_bank{c}", tag=f"bank{CHUNKS + c}")
             second_product(c, [bank[:, a, :] for a in range(OUT_TILES)])
-            sums.append(bank)
-        last_banks = [psum.tile([P, CHUNK], F32, name=f"last_bank{a}", tag=f"bank{a}") for a in range(OUT_TILES)]
+            result = keep.tile([P, OUT_TILES, CHUNK], F32, name=f"result{c}", align_bytes=ALIGN)
+            nc.scalar.copy(out=result[:], in_=bank[:])
+            nc.sync.dma_start(out=out_tiles[:, :, chunks[c]], in_=result[:])
+        last_banks = [psum.tile([P, CHUNK], F32, name=f"last_bank{a}", tag=f"bank{PAIR + a}") for a in range(OUT_TILES)]
         second_product(last, [bank[:] for bank in last_banks])
-        for c in range(last):
-            copy = nc.vector.tensor_copy if c != 1 else nc.scalar.copy
-            copy(out=results[c][:], in_=sums[c][:])
-            nc.sync.dma_start(out=out_tiles[:, :, chunks[c]], in_=results[c][:])
-        nc.vector.tensor_copy(out=results[last][:, 1, :], in_=last_banks[1][:])
-        nc.sync.dma_start(out=out_tiles[:, 1, chunks[last]], in_=results[last][:, 1, :])
-        nc.scalar.copy(out=results[last][:, 0, :], in_=last_banks[0][:])
-        nc.sync.dma_start(out=out_tiles[:, 0, chunks[last]], in_=results[last][:, 0, :])
+        for a, copy in enumerate((nc.vector.tensor_copy, nc.scalar.copy)):
+            result = keep.tile([P, CHUNK], F32, name=f"last_result{a}", align_bytes=ALIGN)
+            copy(out=result[:], in_=last_banks[a][:])
+            nc.sync.dma_start(out=out_tiles[:, a, chunks[last]], in_=result[:])

@@ -41,7 +41,8 @@ def tile_picked_posadd_none_p_kernel(tc, x_words, x_scales, w1, w2, pe, offs, ou
         scale_table = keep.tile([P, T], U8, name="scale_table", align_bytes=ALIGN)
         w1_raw = [keep.tile([P, PACK, H], F32, name=f"w1_raw{z}", align_bytes=ALIGN) for z in range(PASSES)]
         pe_table = [keep.tile([P, T], F32, name=f"pe_table{t}", align_bytes=ALIGN) for t in range(PACK)]
-        w2_raw = keep.tile([P, PACK, N], F32, name="w2_raw", align_bytes=ALIGN)
+        shared = keep.tile([P, CHUNK + PACK * N], F32, name="shared", align_bytes=ALIGN)
+        w2_raw = shared[:, CHUNK:].rearrange("p (j n) -> p j n", j=PACK)
 
         def entries(cols):
             return offsets[:, cols.start // ENTRIES_PER_COLUMN : cols.stop // ENTRIES_PER_COLUMN]
@@ -64,9 +65,8 @@ def tile_picked_posadd_none_p_kernel(tc, x_words, x_scales, w1, w2, pe, offs, ou
             nc.sync.dma_start(out=w1_raw[z][:], in_=w1_rows[z])
         load_x(1)
         for t in range(PACK):
-            if t == PACK - 1:
-                nc.sync.dma_start(out=w2_raw[:], in_=w2.rearrange("(p j) n -> p j n", j=PACK))
             nc.sync.dma_start(out=pe_table[t][:], in_=pe_planes[t])
+        nc.sync.dma_start(out=w2_raw, in_=w2.rearrange("(p j) n -> p j n", j=PACK))
 
         pairs = [slice(0, PAIR), slice(PAIR, PACK)]
         halves = [slice(0, HALF), slice(HALF, S)]
@@ -105,7 +105,7 @@ def tile_picked_posadd_none_p_kernel(tc, x_words, x_scales, w1, w2, pe, offs, ou
         banks = {}
 
         def first_product(u, g):
-            banks[u, g] = psum.tile([P, PAIR, HALF], F32, name=f"plane_bank{u}_{g}", tag=f"bank{g}")
+            banks[u, g] = psum.tile([P, PAIR, HALF], F32, name=f"plane_bank{u}_{g}", tag=f"bank{PAIR * u + g}")
             for z in range(PASSES):
                 for e in range(PAIR):
                     cols = slice((PAIR * u + e) * P, (PAIR * u + e + 1) * P)
@@ -119,14 +119,24 @@ def tile_picked_posadd_none_p_kernel(tc, x_words, x_scales, w1, w2, pe, offs, ou
                         stop=(z == PASSES - 1 and e == PAIR - 1),
                     )
 
-        for g in range(len(halves)):
-            first_product(0, g)
+        for u in range(len(pairs)):
+            for g in range(len(halves)):
+                first_product(u, g)
 
         pe_picked = [keep.tile([P, PAIR, S], F32, name=f"pe_picked{u}", align_bytes=ALIGN) for u in range(len(pairs))]
         h_grouped = [keep.tile([P, CHUNK * PACK], BF16, name=f"h_grouped{c}", align_bytes=ALIGN) for c in range(CHUNKS)]
 
+        last = CHUNKS - 1
+        last_picked = shared[:, : PAIR * CHUNK].rearrange("p (t s) -> p t s", t=PAIR)
+
+        def picked(u, part):
+            return last_picked if (u, part) == (1, chunks[last]) else pe_picked[u][:, :, part]
+
         def pick_pe(t, part):
-            nc.scalar.activation(pe_picked[t // PAIR][:, t % PAIR, part], pe_table[t][:].indirect(entries(part)), COPY)
+            nc.scalar.activation(picked(t // PAIR, part)[:, t % PAIR, :], pe_table[t][:].indirect(entries(part)), COPY)
+
+        def pick_pe_on_vector(t, part):
+            nc.vector.tensor_copy(picked(t // PAIR, part)[:, t % PAIR, :], pe_table[t][:].indirect(entries(part)))
 
         def add_pe(u, c):
             g, first = divmod(c * CHUNK, HALF)
@@ -134,67 +144,81 @@ def tile_picked_posadd_none_p_kernel(tc, x_words, x_scales, w1, w2, pe, offs, ou
             nc.vector.tensor_tensor(
                 h_grouped[c][:].rearrange("p (c i t) -> p c t i", i=RUN, t=PACK)[:, :, pairs[u], :],
                 banks[u, g][:, :, first : first + CHUNK].rearrange(walk, i=RUN),
-                pe_picked[u][:, :, chunks[c]].rearrange(walk, i=RUN),
+                picked(u, chunks[c]).rearrange(walk, i=RUN),
                 ADD,
             )
 
         pick_pe(0, slice(0, S))
-        for part in halves:
-            pick_pe(1, part)
+        pick_pe_on_vector(1, halves[0])
+        pick_pe(1, halves[1])
         for c in range(CHUNKS):
             add_pe(0, c)
-        for g in range(len(halves)):
-            first_product(1, g)
-        pick_pe(2, slice(0, S))
+        pick_pe(2, slice(0, last * CHUNK))
+        pick_pe_on_vector(2, chunks[last])
 
-        w2_grouped = [keep.tile([P, P * PACK], BF16, name=f"w2_grouped{a}", align_bytes=ALIGN) for a in range(OUT_TILES)]
+        out_tiles = out.rearrange("(a p) s -> p a s", p=P)
+        stretches = [halves[0], chunks[2], chunks[3]]
+        h_codes, h_scales = {}, {}
+
+        def quantise_h(c):
+            k = max(c - 1, 0)
+            width = stretches[k].stop - stretches[k].start
+            if k not in h_codes:
+                tag = f"w2_grouped{k - 1}" if k > 0 else "h_codes0"
+                h_codes[k] = keep.tile([P, width], U32, name=f"h_codes{k}", tag=tag, align_bytes=ALIGN)
+                h_scales[k] = keep.tile([P, width], U8, name=f"h_scales{k}", align_bytes=ALIGN)
+            cols = slice(c * CHUNK - stretches[k].start, (c + 1) * CHUNK - stretches[k].start)
+            nc.vector.quantize_mx(out=h_codes[k][:, cols].bitcast(FP8X4), scales=h_scales[k][:, cols], in_=h_grouped[c][:])
+
+        for c in range(last):
+            pick_pe(PACK - 1, chunks[c])
+        w2_grouped = [keep.tile([P, P * PACK], BF16, name=f"w2_grouped{a}", tag=f"w2_grouped{a}", align_bytes=ALIGN) for a in range(OUT_TILES)]
         w2_codes = [keep.tile([P, P], U32, name=f"w2_codes{a}", align_bytes=ALIGN) for a in range(OUT_TILES)]
         w2_scales = [keep.tile([P, P], U8, name=f"w2_scales{a}", align_bytes=ALIGN) for a in range(OUT_TILES)]
-        for a, copy in enumerate((nc.vector.tensor_copy, nc.scalar.copy)):
+
+        def group_w2(copy, a):
             copy(
                 out=w2_grouped[a][:].rearrange("p (c i j) -> p c j i", i=RUN, j=PACK),
                 in_=w2_raw[:, :, a * P : (a + 1) * P].rearrange("p j (c i) -> p c j i", i=RUN),
             )
-        for a in range(OUT_TILES):
+
+        def quantise_w2(a):
             nc.vector.quantize_mx(out=w2_codes[a][:].bitcast(FP8X4), scales=w2_scales[a][:], in_=w2_grouped[a][:])
 
-        out_tiles = out.rearrange("(a p) s -> p a s", p=P)
-        h_codes = [keep.tile([P, CHUNK], U32, name=f"h_codes{c}", align_bytes=ALIGN) for c in range(CHUNKS)]
-        h_scales = [keep.tile([P, CHUNK], U8, name=f"h_scales{c}", align_bytes=ALIGN) for c in range(CHUNKS)]
+        group_w2(nc.scalar.copy, 0)
+        pick_pe(PACK - 1, chunks[last])
+        group_w2(nc.scalar.copy, 1)
+        add_pe(1, 0)
+        add_pe(1, 1)
+        quantise_h(0)
+        add_pe(1, 2)
+        quantise_h(1)
+        quantise_w2(0)
+        add_pe(1, 3)
+        quantise_h(2)
+        quantise_w2(1)
+        quantise_h(3)
 
-        def quantise_h(c):
-            nc.vector.quantize_mx(out=h_codes[c][:].bitcast(FP8X4), scales=h_scales[c][:], in_=h_grouped[c][:])
+        def second_product(a, k, copy):
+            part = stretches[k]
+            width = part.stop - part.start
+            bank = psum.tile([P, width], F32, name=f"out_bank{a}_{k}", tag=f"bank{(CHUNKS + len(stretches) * a + k) % 8}")
+            nc.tensor.matmul_mx(
+                out=bank[:],
+                lhsT=w2_codes[a][:].bitcast(FP8X4),
+                lhsT_scale=w2_scales[a][:],
+                rhs=h_codes[k][:].bitcast(FP8X4),
+                rhs_scale=h_scales[k][:],
+                start=True,
+                stop=True,
+            )
+            result = keep.tile([P, width], F32, name=f"result{a}_{k}", align_bytes=ALIGN)
+            copy(out=result[:], in_=bank[:])
+            nc.sync.dma_start(out=out_tiles[:, a, part], in_=result[:])
 
-        for c in range(CHUNKS):
-            pick_pe(PACK - 1, chunks[c])
-        for c in range(CHUNKS):
-            add_pe(1, c)
-            if c > 0:
-                quantise_h(c - 1)
-        quantise_h(CHUNKS - 1)
-
-        def second_product(c, sums):
-            for a in range(OUT_TILES):
-                nc.tensor.matmul_mx(
-                    out=sums[a],
-                    lhsT=w2_codes[a][:].bitcast(FP8X4),
-                    lhsT_scale=w2_scales[a][:],
-                    rhs=h_codes[c][:].bitcast(FP8X4),
-                    rhs_scale=h_scales[c][:],
-                    start=True,
-                    stop=True,
-                )
-
-        last = CHUNKS - 1
-        for c in range(last):
-            bank = psum.tile([P, OUT_TILES, CHUNK], F32, name=f"out_bank{c}", tag=f"bank{CHUNKS + c}")
-            second_product(c, [bank[:, a, :] for a in range(OUT_TILES)])
-            result = keep.tile([P, OUT_TILES, CHUNK], F32, name=f"result{c}", align_bytes=ALIGN)
-            nc.scalar.copy(out=result[:], in_=bank[:])
-            nc.sync.dma_start(out=out_tiles[:, :, chunks[c]], in_=result[:])
-        last_banks = [psum.tile([P, CHUNK], F32, name=f"last_bank{a}", tag=f"bank{PAIR + a}") for a in range(OUT_TILES)]
-        second_product(last, [bank[:] for bank in last_banks])
-        for a, copy in enumerate((nc.vector.tensor_copy, nc.scalar.copy)):
-            result = keep.tile([P, CHUNK], F32, name=f"last_result{a}", align_bytes=ALIGN)
-            copy(out=result[:], in_=last_banks[a][:])
-            nc.sync.dma_start(out=out_tiles[:, a, chunks[last]], in_=result[:])
+        second_product(0, 0, nc.scalar.copy)
+        second_product(0, 1, nc.scalar.copy)
+        second_product(1, 0, nc.scalar.copy)
+        second_product(1, 1, nc.vector.tensor_copy)
+        second_product(0, 2, nc.vector.tensor_copy)
+        second_product(1, 2, nc.scalar.copy)

@@ -55,14 +55,19 @@ def tile_picked_posadd_none_p_kernel(tc, x_words, x_scales, w1, w2, pe, offs, ou
 
         nc.vector.memset(scale_table[:].bitcast(I32), 0)
         load_x(0)
+
+        def load_scales(z):
+            for r in range(SCALE_ROWS):
+                nc.sync.dma_start(
+                    out=scale_table[SCALE_ROWS * z + r : P : QUADRANT, :].bitcast(I32),
+                    in_=x_scales[z, r::SCALE_ROWS, :].bitcast(I32),
+                )
+
+        load_scales(0)
         nc.sync.dma_start(offsets[:], offs)
-        for q in range(P // QUADRANT):
-            nc.sync.dma_start(
-                out=scale_table[QUADRANT * q : QUADRANT * q + SCALE_ROWS * PASSES, :].bitcast(I32),
-                in_=x_scales[:, SCALE_ROWS * q : SCALE_ROWS * (q + 1), :].bitcast(I32),
-            )
-        for z in range(PASSES):
-            nc.sync.dma_start(out=w1_raw[z][:], in_=w1_rows[z])
+        nc.sync.dma_start(out=w1_raw[0][:], in_=w1_rows[0])
+        load_scales(1)
+        nc.sync.dma_start(out=w1_raw[1][:], in_=w1_rows[1])
         load_x(1)
         for t in range(PACK):
             nc.sync.dma_start(out=pe_table[t][:], in_=pe_planes[t])

@@ -26,6 +26,7 @@ RUN = 4
 CHUNK = 128
 CHUNKS = S // CHUNK
 HALF = S // 2
+LATE = 64
 OUT_TILES = N // P
 ALIGN = 64
 
@@ -40,9 +41,9 @@ def tile_picked_posadd_none_p_kernel(tc, x_words, x_scales, w1, w2, pe, offs, ou
         x_table = [keep.tile([P, T], I32, name=f"x_table{z}", align_bytes=ALIGN) for z in range(PASSES)]
         scale_table = keep.tile([P, T], U8, name="scale_table", align_bytes=ALIGN)
         w1_raw = [keep.tile([P, PACK, H], F32, name=f"w1_raw{z}", align_bytes=ALIGN) for z in range(PASSES)]
-        pe_table = [keep.tile([P, T], F32, name=f"pe_table{t}", align_bytes=ALIGN) for t in range(PACK)]
-        shared = keep.tile([P, CHUNK + PACK * N], F32, name="shared", align_bytes=ALIGN)
-        w2_raw = shared[:, CHUNK:].rearrange("p (j n) -> p j n", j=PACK)
+        pe_table = [keep.tile([P, T], F32, name=f"pe_table{t}", tag=f"pe_table{t}", align_bytes=ALIGN) for t in range(PACK)]
+        shared = keep.tile([P, PAIR * CHUNK - LATE + PACK * N], F32, name="shared", tag="shared", align_bytes=ALIGN)
+        w2_raw = shared[:, PAIR * CHUNK - LATE :].rearrange("p (j n) -> p j n", j=PACK)
 
         def entries(cols):
             return offsets[:, cols.start // ENTRIES_PER_COLUMN : cols.stop // ENTRIES_PER_COLUMN]
@@ -135,7 +136,10 @@ def tile_picked_posadd_none_p_kernel(tc, x_words, x_scales, w1, w2, pe, offs, ou
         last_picked = shared[:, : PAIR * CHUNK].rearrange("p (t s) -> p t s", t=PAIR)
 
         def picked(u, part):
-            return last_picked if (u, part) == (1, chunks[last]) else pe_picked[u][:, :, part]
+            first = chunks[last].start
+            if u == 1 and part.start >= first:
+                return last_picked[:, :, part.start - first : part.stop - first]
+            return pe_picked[u][:, :, part]
 
         def pick_pe(t, part):
             nc.scalar.activation(picked(t // PAIR, part)[:, t % PAIR, :], pe_table[t][:].indirect(entries(part)), COPY)
@@ -154,7 +158,8 @@ def tile_picked_posadd_none_p_kernel(tc, x_words, x_scales, w1, w2, pe, offs, ou
             )
 
         pick_pe(0, slice(0, S))
-        pick_pe_on_vector(1, halves[0])
+        pick_pe_on_vector(1, chunks[0])
+        pick_pe(1, chunks[1])
         pick_pe(1, halves[1])
         for c in range(CHUNKS):
             add_pe(0, c)
@@ -169,7 +174,7 @@ def tile_picked_posadd_none_p_kernel(tc, x_words, x_scales, w1, w2, pe, offs, ou
             k = max(c - 1, 0)
             width = stretches[k].stop - stretches[k].start
             if k not in h_codes:
-                tag = f"w2_grouped{k - 1}" if k > 0 else "h_codes0"
+                tag = ("h_codes0", "pe_table3", "h_codes2")[k]
                 h_codes[k] = keep.tile([P, width], U32, name=f"h_codes{k}", tag=tag, align_bytes=ALIGN)
                 h_scales[k] = keep.tile([P, width], U8, name=f"h_scales{k}", align_bytes=ALIGN)
             cols = slice(c * CHUNK - stretches[k].start, (c + 1) * CHUNK - stretches[k].start)
@@ -177,6 +182,7 @@ def tile_picked_posadd_none_p_kernel(tc, x_words, x_scales, w1, w2, pe, offs, ou
 
         for c in range(last):
             pick_pe(PACK - 1, chunks[c])
+        pick_pe_on_vector(PACK - 1, slice(chunks[last].start, S - LATE))
         w2_grouped = [keep.tile([P, P * PACK], BF16, name=f"w2_grouped{a}", tag=f"w2_grouped{a}", align_bytes=ALIGN) for a in range(OUT_TILES)]
         w2_codes = [keep.tile([P, P], U32, name=f"w2_codes{a}", align_bytes=ALIGN) for a in range(OUT_TILES)]
         w2_scales = [keep.tile([P, P], U8, name=f"w2_scales{a}", align_bytes=ALIGN) for a in range(OUT_TILES)]
@@ -191,17 +197,17 @@ def tile_picked_posadd_none_p_kernel(tc, x_words, x_scales, w1, w2, pe, offs, ou
             nc.vector.quantize_mx(out=w2_codes[a][:].bitcast(FP8X4), scales=w2_scales[a][:], in_=w2_grouped[a][:])
 
         group_w2(nc.scalar.copy, 0)
-        pick_pe(PACK - 1, chunks[last])
         group_w2(nc.scalar.copy, 1)
+        pick_pe(PACK - 1, slice(S - LATE, S))
         add_pe(1, 0)
         add_pe(1, 1)
         quantise_h(0)
         add_pe(1, 2)
         quantise_h(1)
         quantise_w2(0)
+        quantise_w2(1)
         add_pe(1, 3)
         quantise_h(2)
-        quantise_w2(1)
         quantise_h(3)
 
         def second_product(a, k, copy):
@@ -222,8 +228,7 @@ def tile_picked_posadd_none_p_kernel(tc, x_words, x_scales, w1, w2, pe, offs, ou
             nc.sync.dma_start(out=out_tiles[:, a, part], in_=result[:])
 
         second_product(0, 0, nc.scalar.copy)
-        second_product(0, 1, nc.scalar.copy)
         second_product(1, 0, nc.scalar.copy)
-        second_product(1, 1, nc.vector.tensor_copy)
-        second_product(0, 2, nc.vector.tensor_copy)
-        second_product(1, 2, nc.scalar.copy)
+        for k in range(1, len(stretches)):
+            second_product(0, k, nc.vector.tensor_copy)
+            second_product(1, k, nc.scalar.copy)

@@ -29,6 +29,7 @@ HALF = S // 2
 LATE = 64
 OUT_TILES = N // P
 ALIGN = 64
+DMA_ALIGN = 256
 
 
 def tile_picked_posadd_none_p_kernel(tc, x_words, x_scales, w1, w2, pe, offs, out):
@@ -38,11 +39,11 @@ def tile_picked_posadd_none_p_kernel(tc, x_words, x_scales, w1, w2, pe, offs, ou
         psum = ctx.enter_context(tc.psum_pool(name="psum", bufs=1))
 
         offsets = keep.tile([P, S // ENTRIES_PER_COLUMN], U16, name="offsets")
-        x_table = [keep.tile([P, T], I32, name=f"x_table{z}", align_bytes=ALIGN) for z in range(PASSES)]
-        scale_table = keep.tile([P, T], U8, name="scale_table", align_bytes=ALIGN)
-        w1_raw = [keep.tile([P, PACK, H], F32, name=f"w1_raw{z}", align_bytes=ALIGN) for z in range(PASSES)]
-        pe_table = [keep.tile([P, T], F32, name=f"pe_table{t}", tag=f"pe_table{t}", align_bytes=ALIGN) for t in range(PACK)]
-        shared = keep.tile([P, PAIR * CHUNK - LATE + PACK * N], F32, name="shared", tag="shared", align_bytes=ALIGN)
+        x_table = [keep.tile([P, T], I32, name=f"x_table{z}", align_bytes=DMA_ALIGN) for z in range(PASSES)]
+        scale_table = keep.tile([P, T], U8, name="scale_table", align_bytes=DMA_ALIGN)
+        w1_raw = [keep.tile([P, PACK, H], F32, name=f"w1_raw{z}", align_bytes=DMA_ALIGN) for z in range(PASSES)]
+        pe_table = [keep.tile([P, T], F32, name=f"pe_table{t}", tag=f"pe_table{t}", align_bytes=DMA_ALIGN) for t in range(PACK)]
+        shared = keep.tile([P, PAIR * CHUNK - LATE + PACK * N], F32, name="shared", tag="shared", align_bytes=DMA_ALIGN)
         w2_raw = shared[:, PAIR * CHUNK - LATE :].rearrange("p (j n) -> p j n", j=PACK)
 
         def entries(cols):
@@ -175,7 +176,7 @@ def tile_picked_posadd_none_p_kernel(tc, x_words, x_scales, w1, w2, pe, offs, ou
             width = stretches[k].stop - stretches[k].start
             if k not in h_codes:
                 tag = ("h_codes0", "pe_table3", "h_codes2")[k]
-                h_codes[k] = keep.tile([P, width], U32, name=f"h_codes{k}", tag=tag, align_bytes=ALIGN)
+                h_codes[k] = keep.tile([P, width], U32, name=f"h_codes{k}", tag=tag, align_bytes=DMA_ALIGN)
                 h_scales[k] = keep.tile([P, width], U8, name=f"h_scales{k}", align_bytes=ALIGN)
             cols = slice(c * CHUNK - stretches[k].start, (c + 1) * CHUNK - stretches[k].start)
             nc.vector.quantize_mx(out=h_codes[k][:, cols].bitcast(FP8X4), scales=h_scales[k][:, cols], in_=h_grouped[c][:])
@@ -223,7 +224,7 @@ def tile_picked_posadd_none_p_kernel(tc, x_words, x_scales, w1, w2, pe, offs, ou
                 start=True,
                 stop=True,
             )
-            result = keep.tile([P, width], F32, name=f"result{a}_{k}", align_bytes=ALIGN)
+            result = keep.tile([P, width], F32, name=f"result{a}_{k}", align_bytes=DMA_ALIGN)
             copy(out=result[:], in_=bank[:])
             nc.sync.dma_start(out=out_tiles[:, a, part], in_=result[:])
 

@@ -58,17 +58,18 @@ def tile_picked_posadd_none_p_kernel(tc, x_words, x_scales, w1, w2, pe, offs, ou
         nc.vector.memset(scale_table[:].bitcast(I32), 0)
         load_x(0)
 
-        def load_scales(z):
-            for r in range(SCALE_ROWS):
-                nc.sync.dma_start(
-                    out=scale_table[SCALE_ROWS * z + r : P : QUADRANT, :].bitcast(I32),
-                    in_=x_scales[z, r::SCALE_ROWS, :].bitcast(I32),
-                )
+        def load_scales(rows):
+            for r in rows:
+                for z in range(PASSES):
+                    nc.sync.dma_start(
+                        out=scale_table[SCALE_ROWS * z + r : P : QUADRANT, :].bitcast(I32),
+                        in_=x_scales[z, r::SCALE_ROWS, :].bitcast(I32),
+                    )
 
-        load_scales(0)
+        load_scales(range(0, SCALE_ROWS // 2))
         nc.sync.dma_start(offsets[:], offs)
         nc.sync.dma_start(out=w1_raw[0][:], in_=w1_rows[0])
-        load_scales(1)
+        load_scales(range(SCALE_ROWS // 2, SCALE_ROWS))
         nc.sync.dma_start(out=w1_raw[1][:], in_=w1_rows[1])
         load_x(1)
         for t in range(PACK):

@@ -112,24 +112,27 @@ def tile_picked_posadd_none_p_kernel(tc, x_words, x_scales, w1, w2, pe, offs, ou
 
         banks = {}
 
-        def first_product(u, g):
-            banks[u, g] = psum.tile([P, PAIR, HALF], F32, name=f"plane_bank{u}_{g}", tag=f"bank{PAIR * u + g}")
+        def first_product(u, part, tag):
+            bank = psum.tile([P, PAIR, part.stop - part.start], F32, name=f"plane_bank{u}_{part.start}", tag=tag)
+            for c in range(part.start // CHUNK, part.stop // CHUNK):
+                banks[u, c] = bank[:, :, c * CHUNK - part.start : (c + 1) * CHUNK - part.start]
             for z in range(PASSES):
                 for e in range(PAIR):
                     cols = slice((PAIR * u + e) * P, (PAIR * u + e + 1) * P)
                     nc.tensor.matmul_mx(
-                        out=banks[u, g][:, e, :],
+                        out=bank[:, e, :],
                         lhsT=w1_codes[z][:, cols].bitcast(FP8X4),
                         lhsT_scale=w1_scales[z][:, cols],
-                        rhs=x_codes[z][:, halves[g]].bitcast(FP8X4),
-                        rhs_scale=x_picked_scales[SCALE_ROWS * z :, halves[g]],
+                        rhs=x_codes[z][:, part].bitcast(FP8X4),
+                        rhs_scale=x_picked_scales[SCALE_ROWS * z :, part],
                         start=(z == 0 and e == 0),
                         stop=(z == PASSES - 1 and e == PAIR - 1),
                     )
 
-        for u in range(len(pairs)):
-            for g in range(len(halves)):
-                first_product(u, g)
+        for g in range(len(halves)):
+            first_product(0, halves[g], f"bank{g}")
+        for c in range(PAIR):
+            first_product(1, chunks[c], f"bank{PAIR + c}")
 
         pe_picked = [keep.tile([P, PAIR, S], F32, name=f"pe_picked{u}", align_bytes=ALIGN) for u in range(len(pairs))]
         h_grouped = [keep.tile([P, CHUNK * PACK], BF16, name=f"h_grouped{c}", align_bytes=ALIGN) for c in range(CHUNKS)]
@@ -150,11 +153,10 @@ def tile_picked_posadd_none_p_kernel(tc, x_words, x_scales, w1, w2, pe, offs, ou
             nc.vector.tensor_copy(picked(t // PAIR, part)[:, t % PAIR, :], pe_table[t][:].indirect(entries(part)))
 
         def add_pe(u, c):
-            g, first = divmod(c * CHUNK, HALF)
             walk = "p t (c i) -> p c t i"
             nc.vector.tensor_tensor(
                 h_grouped[c][:].rearrange("p (c i t) -> p c t i", i=RUN, t=PACK)[:, :, pairs[u], :],
-                banks[u, g][:, :, first : first + CHUNK].rearrange(walk, i=RUN),
+                banks[u, c].rearrange(walk, i=RUN),
                 picked(u, chunks[c]).rearrange(walk, i=RUN),
                 ADD,
             )
@@ -165,6 +167,7 @@ def tile_picked_posadd_none_p_kernel(tc, x_words, x_scales, w1, w2, pe, offs, ou
         pick_pe(1, halves[1])
         for c in range(CHUNKS):
             add_pe(0, c)
+        first_product(1, chunks[2], "bank1")
         pick_pe(2, slice(0, last * CHUNK))
         pick_pe_on_vector(2, chunks[last])
 
@@ -202,6 +205,7 @@ def tile_picked_posadd_none_p_kernel(tc, x_words, x_scales, w1, w2, pe, offs, ou
         group_w2(nc.scalar.copy, 1)
         pick_pe(PACK - 1, slice(S - LATE, S))
         add_pe(1, 0)
+        first_product(1, chunks[3], "bank2")
         add_pe(1, 1)
         quantise_h(0)
         add_pe(1, 2)
@@ -215,7 +219,7 @@ def tile_picked_posadd_none_p_kernel(tc, x_words, x_scales, w1, w2, pe, offs, ou
         def second_product(a, k, copy):
             part = stretches[k]
             width = part.stop - part.start
-            bank = psum.tile([P, width], F32, name=f"out_bank{a}_{k}", tag=f"bank{(CHUNKS + len(stretches) * a + k) % 8}")
+            bank = psum.tile([P, width], F32, name=f"out_bank{a}_{k}", tag=f"bank{(CHUNKS + OUT_TILES * k + a) % 8}")
             nc.tensor.matmul_mx(
                 out=bank[:],
                 lhsT=w2_codes[a][:].bitcast(FP8X4),

from contextlib import ExitStack

import concourse.mybir as mybir

K, T, S, H, N = 1024, 1024, 512, 512, 256
FLOPS = 2 * K * H * S + 2 * H * N * S

F32 = mybir.dt.float32
BF16 = mybir.dt.bfloat16
I32 = mybir.dt.int32
U32 = mybir.dt.uint32
U16 = mybir.dt.uint16
U8 = mybir.dt.uint8
FP8X4 = mybir.dt.float8_e4m3fn_x4
ADD = mybir.AluOpType.add
COPY = mybir.ActivationFunctionType.Copy

P = 128
PACK = 4
PAIR = 2
PASSES = K // (P * PACK)
QUADRANT = 32
SCALE_ROWS = 4
ENTRIES_PER_COLUMN = 16
RUN = 4
CHUNK = 128
CHUNKS = S // CHUNK
HALF = S // 2
LATE = 64
OUT_TILES = N // P
ALIGN = 64
DMA_ALIGN = 256


def tile_picked_posadd_none_p_kernel(tc, x_words, x_scales, w1, w2, pe, offs, out):
    nc = tc.nc
    with ExitStack() as ctx:
        keep = ctx.enter_context(tc.tile_pool(name="keep", bufs=1))
        psum = ctx.enter_context(tc.psum_pool(name="psum", bufs=1))

        offsets = keep.tile([P, S // ENTRIES_PER_COLUMN], U16, name="offsets")
        x_table = [keep.tile([P, T], I32, name=f"x_table{z}", align_bytes=DMA_ALIGN) for z in range(PASSES)]
        scale_table = keep.tile([P, T], U8, name="scale_table", align_bytes=DMA_ALIGN)
        w1_raw = [keep.tile([P, PACK, H], F32, name=f"w1_raw{z}", align_bytes=DMA_ALIGN) for z in range(PASSES)]
        pe_table = [keep.tile([P, T], F32, name=f"pe_table{t}", tag=f"pe_table{t}", align_bytes=DMA_ALIGN) for t in range(PACK)]
        shared = keep.tile([P, PAIR * CHUNK - LATE + PACK * N], F32, name="shared", tag="shared", align_bytes=DMA_ALIGN)
        w2_raw = shared[:, PAIR * CHUNK - LATE :].rearrange("p (j n) -> p j n", j=PACK)

        def entries(cols):
            return offsets[:, cols.start // ENTRIES_PER_COLUMN : cols.stop // ENTRIES_PER_COLUMN]

        def load_x(z):
            nc.sync.dma_start(out=x_table[z][:], in_=x_words[z].rearrange("p c r -> p (c r)").bitcast(I32))

        w1_rows = w1.rearrange("(z p j) c -> z p j c", z=PASSES, j=PACK)
        pe_planes = pe.rearrange("(p t) c -> t p c", t=PACK)

        nc.vector.memset(scale_table[:].bitcast(I32), 0)
        load_x(0)

        def load_scales(rows):
            for r in rows:
                for z in range(PASSES):
                    nc.sync.dma_start(
                        out=scale_table[SCALE_ROWS * z + r : P : QUADRANT, :].bitcast(I32),
                        in_=x_scales[z, r::SCALE_ROWS, :].bitcast(I32),
                    )

        load_scales(range(0, SCALE_ROWS // 2))
        nc.sync.dma_start(offsets[:], offs)
        nc.sync.dma_start(out=w1_raw[0][:], in_=w1_rows[0])
        load_scales(range(SCALE_ROWS // 2, SCALE_ROWS))
        nc.sync.dma_start(out=w1_raw[1][:], in_=w1_rows[1])
        load_x(1)
        for t in range(PACK):
            nc.sync.dma_start(out=pe_table[t][:], in_=pe_planes[t])
        nc.sync.dma_start(out=w2_raw, in_=w2.rearrange("(p j) n -> p j n", j=PACK))

        pairs = [slice(0, PAIR), slice(PAIR, PACK)]
        halves = [slice(0, HALF), slice(HALF, S)]
        chunks = [slice(c * CHUNK, (c + 1) * CHUNK) for c in range(CHUNKS)]
        w1_codes = [keep.tile([P, H], U32, name=f"w1_codes{z}", align_bytes=ALIGN) for z in range(PASSES)]
        w1_scales = [keep.tile([P, H], U8, name=f"w1_scales{z}", align_bytes=ALIGN) for z in range(PASSES)]
        w1_grouped = [
            [keep.tile([P, PAIR, P, PACK], BF16, name=f"w1_grouped{z}_{u}", align_bytes=ALIGN) for u in range(len(pairs))]
            for z in range(PASSES)
        ]

        def group_w1(copy, z, u):
            src = w1_raw[z][:].rearrange("p j (m t) -> p m j t", t=PACK)
            copy(out=w1_grouped[z][u][:].rearrange("p t m j -> p m j t"), in_=src[:, :, :, pairs[u]])

        def quantise_w1(z, u):
            cols = slice(pairs[u].start * P, pairs[u].stop * P)
            nc.vector.quantize_mx(
                out=w1_codes[z][:, cols].bitcast(FP8X4),
                scales=w1_scales[z][:, cols],
                in_=w1_grouped[z][u][:].rearrange("p t m j -> p (t m j)"),
            )

        x_codes = [keep.tile([P, S], U32, name=f"x_codes{z}", align_bytes=ALIGN) for z in range(PASSES)]
        x_picked_scales = keep.tile([P, S], U8, name="x_picked_scales", align_bytes=ALIGN)
        nc.vector.tensor_copy(x_codes[0][:], x_table[0][:].bitcast(U32).indirect(offsets[:]))
        nc.vector.tensor_copy(x_picked_scales[:], scale_table[:].indirect(offsets[:]))
        for z in range(PASSES):
            group_w1(nc.vector.tensor_copy, z, 0)
            group_w1(nc.scalar.copy, z, 1)
            for u in range(len(pairs)):
                quantise_w1(z, u)
        for part in halves:
            nc.vector.tensor_copy(x_codes[1][:, part], x_table[1][:].bitcast(U32).indirect(entries(part)))

        banks = {}

        def first_product(u, part, tag):
            bank = psum.tile([P, PAIR, part.stop - part.start], F32, name=f"plane_bank{u}_{part.start}", tag=tag)
            for c in range(part.start // CHUNK, part.stop // CHUNK):
                banks[u, c] = bank[:, :, c * CHUNK - part.start : (c + 1) * CHUNK - part.start]
            for z in range(PASSES):
                for e in range(PAIR):
                    cols = slice((PAIR * u + e) * P, (PAIR * u + e + 1) * P)
                    nc.tensor.matmul_mx(
                        out=bank[:, e, :],
                        lhsT=w1_codes[z][:, cols].bitcast(FP8X4),
                        lhsT_scale=w1_scales[z][:, cols],
                        rhs=x_codes[z][:, part].bitcast(FP8X4),
                        rhs_scale=x_picked_scales[SCALE_ROWS * z :, part],
                        start=(z == 0 and e == 0),
                        stop=(z == PASSES - 1 and e == PAIR - 1),
                    )

        for g in range(len(halves)):
            first_product(0, halves[g], f"bank{g}")
        for c in range(PAIR):
            first_product(1, chunks[c], f"bank{PAIR + c}")

        pe_picked = [keep.tile([P, PAIR, S], F32, name=f"pe_picked{u}", align_bytes=ALIGN) for u in range(len(pairs))]
        h_grouped = [keep.tile([P, CHUNK * PACK], BF16, name=f"h_grouped{c}", align_bytes=ALIGN) for c in range(CHUNKS)]

        last = CHUNKS - 1
        last_picked = shared[:, : PAIR * CHUNK].rearrange("p (t s) -> p t s", t=PAIR)

        def picked(u, part):
            first = chunks[last].start
            if u == 1 and part.start >= first:
                return last_picked[:, :, part.start - first : part.stop - first]
            return pe_picked[u][:, :, part]

        def pick_pe(t, part):
            nc.scalar.activation(picked(t // PAIR, part)[:, t % PAIR, :], pe_table[t][:].indirect(entries(part)), COPY)

        def pick_pe_on_vector(t, part):
            nc.vector.tensor_copy(picked(t // PAIR, part)[:, t % PAIR, :], pe_table[t][:].indirect(entries(part)))

        def add_pe(u, c):
            walk = "p t (c i) -> p c t i"
            nc.vector.tensor_tensor(
                h_grouped[c][:].rearrange("p (c i t) -> p c t i", i=RUN, t=PACK)[:, :, pairs[u], :],
                banks[u, c].rearrange(walk, i=RUN),
                picked(u, chunks[c]).rearrange(walk, i=RUN),
                ADD,
            )

        pick_pe(0, slice(0, S))
        pick_pe_on_vector(1, chunks[0])
        pick_pe(1, chunks[1])
        pick_pe(1, halves[1])
        for c in range(CHUNKS):
            add_pe(0, c)
        first_product(1, chunks[2], "bank1")
        pick_pe(2, slice(0, last * CHUNK))
        pick_pe_on_vector(2, chunks[last])

        out_tiles = out.rearrange("(a p) s -> p a s", p=P)
        stretches = [halves[0], chunks[2], chunks[3]]
        h_codes, h_scales = {}, {}

        def quantise_h(c):
            k = max(c - 1, 0)
            width = stretches[k].stop - stretches[k].start
            if k not in h_codes:
                tag = ("h_codes0", "pe_table3", "h_codes2")[k]
                h_codes[k] = keep.tile([P, width], U32, name=f"h_codes{k}", tag=tag, align_bytes=DMA_ALIGN)
                h_scales[k] = keep.tile([P, width], U8, name=f"h_scales{k}", align_bytes=ALIGN)
            cols = slice(c * CHUNK - stretches[k].start, (c + 1) * CHUNK - stretches[k].start)
            nc.vector.quantize_mx(out=h_codes[k][:, cols].bitcast(FP8X4), scales=h_scales[k][:, cols], in_=h_grouped[c][:])

        for c in range(last):
            pick_pe(PACK - 1, chunks[c])
        pick_pe_on_vector(PACK - 1, slice(chunks[last].start, S - LATE))
        w2_grouped = [keep.tile([P, P * PACK], BF16, name=f"w2_grouped{a}", tag=f"w2_grouped{a}", align_bytes=ALIGN) for a in range(OUT_TILES)]
        w2_codes = [keep.tile([P, P], U32, name=f"w2_codes{a}", align_bytes=ALIGN) for a in range(OUT_TILES)]
        w2_scales = [keep.tile([P, P], U8, name=f"w2_scales{a}", align_bytes=ALIGN) for a in range(OUT_TILES)]

        def group_w2(copy, a):
            copy(
                out=w2_grouped[a][:].rearrange("p (c i j) -> p c j i", i=RUN, j=PACK),
                in_=w2_raw[:, :, a * P : (a + 1) * P].rearrange("p j (c i) -> p c j i", i=RUN),
            )

        def quantise_w2(a):
            nc.vector.quantize_mx(out=w2_codes[a][:].bitcast(FP8X4), scales=w2_scales[a][:], in_=w2_grouped[a][:])

        group_w2(nc.scalar.copy, 0)
        group_w2(nc.scalar.copy, 1)
        pick_pe(PACK - 1, slice(S - LATE, S))
        add_pe(1, 0)
        first_product(1, chunks[3], "bank2")
        add_pe(1, 1)
        quantise_h(0)
        add_pe(1, 2)
        quantise_h(1)
        quantise_w2(0)
        quantise_w2(1)
        add_pe(1, 3)
        quantise_h(2)
        quantise_h(3)

        def second_product(a, k, copy):
            part = stretches[k]
            width = part.stop - part.start
            bank = psum.tile([P, width], F32, name=f"out_bank{a}_{k}", tag=f"bank{(CHUNKS + OUT_TILES * k + a) % 8}")
            nc.tensor.matmul_mx(
                out=bank[:],
                lhsT=w2_codes[a][:].bitcast(FP8X4),
                lhsT_scale=w2_scales[a][:],
                rhs=h_codes[k][:].bitcast(FP8X4),
                rhs_scale=h_scales[k][:],
                start=True,
                stop=True,
            )
            result = keep.tile([P, width], F32, name=f"result{a}_{k}", align_bytes=DMA_ALIGN)
            copy(out=result[:], in_=bank[:])
            nc.sync.dma_start(out=out_tiles[:, a, part], in_=result[:])

        second_product(0, 0, nc.scalar.copy)
        second_product(1, 0, nc.scalar.copy)
        for k in range(1, len(stretches)):
            second_product(0, k, nc.vector.tensor_copy)
            second_product(1, k, nc.scalar.copy)
